import numpy as np, ml_dtypes
CORES = [35,38,43,46]
N = 4
BF = ml_dtypes.bfloat16
def gentries(a):
    return np.ascontiguousarray(a.reshape(8, 16, -1).transpose(0, 2, 1)).reshape(8, -1)
def gtable(e):
    e = np.asarray(e); return np.ascontiguousarray(e.reshape(8, -1, 16).transpose(0, 2, 1)).reshape(128, -1).astype(np.int32)
W, F, FC, LM, CAP, TS, LB, RO = 3456, 256, 512, 32, 64, 2048, 2, 3
WT = 255 - 14 * np.arange(16)
M = 8
def pick(t, ix):
    return np.take_along_axis(t, ix[:, :, None, :], 3)
def letters(rng, uneven):
    C = W // M; A = C // 4; hc = (A // 2) * 4; hw = hc * M
    if uneven:
        v = (np.floor(np.exp2(8 * rng.random((N, 8, 1, C))) * rng.random((N, 8, 16, C))) * (rng.random((N, 8, 1, C)) > 0.0625)).astype(np.int64)
        q = (np.floor(np.exp2(8 * rng.random((N, 8, 1, W))) * rng.random((N, 8, 16, W))) * (rng.random((N, 8, 1, W)) > 0.0625)).astype(np.int64)
    else:
        v = rng.integers(0, 256, (N, 8, 16, C)); q = rng.integers(0, 256, (N, 8, 16, W))
    base = rng.integers(0, C, (N, 8, A, 16)); base[:, :, :A // 2] %= hc
    alt = rng.integers(0, C, (N, 8, C, 16)); alt[:, :, :hc] %= hc
    seq = np.repeat(base, 4, axis=2); seq = np.where(rng.random(seq.shape) < 0.08, alt, seq)
    blk = np.repeat(np.add.accumulate((rng.random((N, 8, A, 16)) < 0.6).astype(np.int64), axis=3), 4 * M, axis=2)
    loose = np.take_along_axis(rng.random((N, 8, W, 17)), blk, 3) < rng.choice(np.array([0.15, 0.3, 0.5]), (N, 8, 1, 1))
    order = np.argsort(blk + np.where(loose, rng.random(blk.shape), 0.0625 * np.arange(16)), axis=3)
    mem = np.repeat(rng.integers(0, M, (N, 8, A, 16)), 4 * M, axis=2)
    mem = np.where(rng.random(mem.shape) < rng.choice(np.array([0.02, 0.06, 0.15, 0.4]), (N, 8, 1, 1)), rng.integers(0, M, mem.shape), mem)
    kid = np.take_along_axis(np.repeat(seq, M, axis=2) * M + mem, order, 3)
    v[:, :, :, :hc] = v[:1, :, :, :hc].copy(); q[:, :, :, :hw] = q[:1, :, :, :hw].copy(); kid[:, :, :hw] = kid[:1, :, :hw].copy()
    return np.repeat(v, M, axis=3), q, kid
def front(rng, skew):
    A = W // (4 * M)
    st = rng.random((N, 8, F)) < rng.choice(np.array([0.3, 0.5, 0.8]), (N, 8, 1)); st[:, :, 0] = True
    st = st.astype(np.int64); sid = np.add.accumulate(st, axis=2) - 1
    fam = (A * rng.random((N, 8, F)) ** (3 if skew else 1)).astype(np.int64)
    fam = np.take_along_axis(np.where(rng.random(fam.shape) < 0.7, fam % (A // 2), fam), sid, 2)
    c = fam * 4 + rng.integers(0, 4, fam.shape); m = rng.integers(0, M, fam.shape)
    o = np.argsort(sid + 0.99 * rng.random(fam.shape), axis=2)
    mv = np.where(rng.random(fam.shape) < 0.3, np.take_along_axis(m, o, 2), rng.integers(0, M, fam.shape))
    fv = np.take_along_axis(c, o, 2) * M + mv
    return c * M + m, np.where(rng.random(fam.shape) < 0.04, rng.integers(0, W, fam.shape), fv), st
def mix(rng, v, q, kid, fu, fv):
    pm = np.argsort(rng.random((N, 8, W)), axis=2); inv = np.argsort(pm, axis=2)
    k = np.take_along_axis(pm, kid.reshape(N, 8, 16 * W), 2).reshape(N, 8, W, 16)
    k = np.ascontiguousarray(np.take_along_axis(k, inv[:, :, :, None], 2).transpose(0, 1, 3, 2))
    return pick(v, inv), pick(q, inv), k, np.take_along_axis(pm, fu, 2), np.take_along_axis(pm, fv, 2)
def pack(v, q, k, fu, fv, st):
    return {"vec": v.reshape(N, 128, W).astype(np.float32).astype(BF), "mark": q.reshape(N, 128, W).astype(np.float32).astype(BF), "kids": np.ascontiguousarray(k.reshape(N, 128, W)).astype(np.int32),
            "fu": np.stack([gtable(a) for a in fu]), "fv": np.stack([gtable(a) for a in fv]), "fs": np.ascontiguousarray(st).astype(np.int32)}
def setup_inputs(rng):
    v, q, kid = letters(rng, False); fu, fv, st = front(rng, False)
    return pack(*mix(rng, v, q, kid, fu, fv), st)
def setup_inputs_room(rng):
    v = np.zeros((N, 8, 16, W), np.int64); q = np.zeros((N, 8, 16, W), np.int64); k = np.zeros((N, 8, 16, W), np.int64)
    fu = np.zeros((N, 8, F), np.int64); fv = np.zeros((N, 8, F), np.int64); st = np.zeros((N, 8, F), np.int64); st[:, :, 0] = 1
    for r in range(N):
        for g in range(8):
            o = rng.permutation(W); z0 = o[2 * F]; rest = o[2 * F + 1:]
            b = rng.integers(0, 2, W); b[z0] = 0; i = int(rng.integers(0, 16))
            v[r, g] = rng.integers(0, 128, (16, 1)); v[r, g, i] += b * int(rng.integers(1, 128))
            own = rng.integers(0, N, W); w = rng.integers(0, 256, (16, W)); w[0] -= w[0] % N; w[0] += (WT @ w - own) % N; w[:, z0] = 0; q[r, g] = w
            pool = [rest[(own[rest] == a) & (b[rest] == 0)] for a in range(N)]; zero = rest[b[rest] == 0]; ones = rest[b[rest] == 1]
            pu = rng.choice(rest, 16 * F); pv = pu.copy(); mode = g if g in (2, 3) else (0, 1, 0, 4)[(r + g) % 4]
            if mode in (0, 1):
                if mode == 0:
                    n = rng.choice(np.array([0, 1, CAP - 1, CAP, CAP + 1, CAP + 8]), N)
                    if r == 0: n[1] = CAP
                    x = rng.permutation(np.concatenate([np.resize(rng.permutation(pool[a]), int(n[a])) for a in range(N)]))
                else:
                    a = rng.permutation(N)
                    x = np.concatenate([np.resize(rng.permutation(pool[a[0]]), FC - 2), np.resize(rng.permutation(pool[a[1]]), 5)])
                t = np.sort(rng.permutation(16 * F)[:len(x)])
                pu[t] = x; pv[t] = z0
            elif mode in (2, 3):
                t = int(rng.integers(0, 8))
                for n in ([LM + 1] + [LM] * (F // LM) + [1] if mode == 2 else [LM] * (F // LM - 1) + [LM - 1, 2, 1, 1]):
                    if n == 1:
                        pu[t] = rng.choice(zero); pv[t] = z0
                    else:
                        pu[t] = rng.choice(zero); pv[t] = rng.choice(ones); pu[t + n - 1] = rng.choice(ones); pv[t + n - 1] = rng.choice(zero)
                    t += n + int(rng.integers(0, 4))
            else:
                lu, lv, lx, ly = int(o[0]), int(o[F]), int(rest[0]), int(rest[1])
                j = 13 if r == 0 else 0 if r == 1 else int(rng.integers(0, 14))
                for c in (lv, lx, ly): v[r, g, :, c] = v[r, g, :, lu]
                q[r, g, j:j + 3, lu] = np.minimum(np.maximum(q[r, g, j:j + 3, lu], 2), 254)
                q[r, g, :, lx] = q[r, g, :, lu]; q[r, g, j:j + 3, lx] += np.array([1, -2, 1])
                q[r, g, :, lv] = 0; q[r, g, :, ly] = 0
                pu[0] = lu; pv[0] = lv; pu[1] = lx; pv[1] = ly
            kk = rng.choice(rest, (16, W)); kk[:, o[:F]] = pu.reshape(F, 16).T; kk[:, o[F:2 * F]] = pv.reshape(F, 16).T
            k[r, g] = kk; fu[r, g] = o[:F]; fv[r, g] = o[F:2 * F]
    return pack(v, q, k, fu, fv, st)
def swing(rng, pu, pv, t, n, low, high):
    x, y = (pu, pv) if rng.random() < 0.5 else (pv, pu)
    x[t] = rng.choice(low); y[t] = rng.choice(high); x[t + n - 1] = rng.choice(high); y[t + n - 1] = rng.choice(low)
def setup_inputs_deep(rng):
    v = np.zeros((N, 8, 16, W), np.int64); q = np.zeros((N, 8, 16, W), np.int64); k = np.zeros((N, 8, 16, W), np.int64)
    fu = np.zeros((N, 8, F), np.int64); fv = np.zeros((N, 8, F), np.int64); st = np.zeros((N, 8, F), np.int64); st[:, :, 0] = 1
    P = 16 * F; C = (LM + 15) // 16
    for r in range(N):
        for g in range(8):
            mode = (r + g) % 4; o = rng.permutation(W); z0 = int(o[2 * F]); rest = o[2 * F + 1:]
            b = rng.integers(0, 3, W) if mode > 1 else rng.integers(0, 2, W) * mode
            b[z0] = 0
            half = 8 * int(rng.integers(0, 2)); m = rng.random((16, 1)) < 0.4; m[np.arange(16) // 8 * 8 != half] = False; m[half + int(rng.integers(0, 8))] = True
            j = 8 - half + int(rng.integers(0, 6)); tri = np.zeros((16, 1), np.int64); tri[j:j + 3, 0] = int(rng.integers(1, 33)) * np.array([1, -2, 1])
            two = m.astype(np.int64) if mode == 2 else tri
            v[r, g] = np.where(m, 0, rng.integers(64, 128, (16, 1))) + 255 * m.astype(np.int64) * (b == 1) + two * (b == 2)
            own = rng.integers(0, N, W); w = rng.integers(0, 256, (16, W)); w[0] -= w[0] % N; w[0] += (WT @ w - own) % N; w[:, z0] = 0; q[r, g] = w
            pool = [rest[(own[rest] == a) & (b[rest] == 0)] for a in range(N)]; kind = [rest[b[rest] == c] for c in range(3)]
            pu = rng.choice(rest, P); pv = pu.copy(); kk = rng.choice(rest, (16, W)); a = rng.permutation(N); a0 = int(a[0]); a1 = int(a[1])
            if mode == 0:
                heads = rest[:64]; t = np.sort(rng.permutation(P)[:64]); pu[t] = heads; pv[t] = z0
                n0 = FC // 16 + (16 if g < 4 else 0)
                kk[:, z0] = z0; kk[:, heads[:n0]] = rng.choice(pool[a0], (16, n0)); kk[:, heads[n0:]] = rng.choice(pool[a1], (16, 64 - n0))
            elif mode == 1:
                t = int(rng.integers(0, 4))
                for n in range(8):
                    swing(rng, pu, pv, t, LM + 1, kind[0], kind[1]); t += LM + 1 + int(rng.integers(0, 4))
                x = np.concatenate([np.resize(rng.permutation(pool[a0]), FC - 16), np.resize(rng.permutation(pool[a1]), 20)])
                i = t + np.sort(rng.permutation(P - t)[:len(x)]); pu[i] = x; pv[i] = z0
            elif mode == 2:
                x, y = (pu, pv) if r % 2 == 0 else (pv, pu)
                t = int(rng.integers(0, 8))
                x[t:t + 257] = rng.choice(kind[1], 257); x[t + 257] = rng.choice(kind[2]); y[t:t + 258] = rng.choice(kind[0], 258); t += 258
                i = t + np.sort(rng.permutation(800)[:24]); pu[i] = rng.choice(kind[0], 24); pv[i] = z0; t += 800
                y[t:t + 257] = rng.choice(kind[1], 257); y[t + 257] = rng.choice(kind[2]); x[t:t + 258] = rng.choice(kind[0], 258); t += 258
                while t + LM + 16 < P:
                    t += int(rng.integers(0, 16)); n = int(rng.integers(2, LM + 1))
                    swing(rng, pu, pv, t, n, kind[0], kind[int(rng.integers(1, 3))]); t += n
            else:
                s = int(rng.integers(1, 6)); e = F - 4 * C
                st[r, g, s] = 1; st[r, g, e + C * np.arange(4)] = 1
                i = int(rng.integers(0, 16 * s)); pu[i] = rng.choice(kind[0]); pv[i] = rng.choice(kind[1])
                t = 16 * s
                while t + LM + 48 < 16 * e:
                    t += int(rng.integers(0, 48))
                    if rng.random() < 0.5:
                        pu[t] = rng.choice(kind[0]); pv[t] = z0; t += 1
                    else:
                        n = int(rng.integers(2, LM + 1)); swing(rng, pu, pv, t, n, kind[0], kind[2]); t += n
                for c in range(4):
                    i = 16 * (e + C * (c + 1)); x, y = (pv, pu) if c < 3 else (pu, pv)
                    x[i - LM:i] = rng.choice(kind[1], LM); y[i - LM:i] = rng.choice(kind[0], LM)
            kk[:, o[:F]] = pu.reshape(F, 16).T; kk[:, o[F:2 * F]] = pv.reshape(F, 16).T
            k[r, g] = kk; fu[r, g] = o[:F]; fv[r, g] = o[F:2 * F]
    return pack(v, q, k, fu, fv, st)
def setup_inputs_ends(rng):
    v, q, kid = letters(rng, False); fu, fv, st = front(rng, False)
    v, q, k, fu, fv = mix(rng, v, q, kid, fu, fv)
    st[:, 0] = 1; st[:, 1] = 0
    two = np.array([0, W - 1]); few = np.array([0, 1, W - 1])
    fu[:, 2] = rng.choice(two, (N, F)); fv[:, 2] = rng.choice(two, (N, F)); k[:, 2, :, 0] = rng.choice(few, (N, 16)); k[:, 2, :, W - 1] = rng.choice(few, (N, 16))
    for r in range(N):
        i = int(rng.integers(0, 16)); x = v[r, 3, i].copy(); v[r, 3] = 7; v[r, 3, i] = x
    v[:, 4] = 255 * (np.arange(W) >= W // 2); k[:, 4] = rng.integers(0, W // 2, (N, 16, W)) + (W // 2) * (np.arange(W) % 2 == 0)
    even = 2 * rng.integers(0, W // 2, (N, F)); odd = 2 * rng.integers(0, W // 2, (N, F)) + 1
    fu[:, 4] = even; fv[:, 4] = odd; fu[1::2, 4] = odd[1::2]; fv[1::2, 4] = even[1::2]; st[:, 4] = 0; st[:, 4, F - 4:] = 1
    fv[:, 5] = rng.integers(0, W, (N, F)); st[:, 5] = np.arange(F) % 3 != 1
    fv[:, 6] = fu[:, 6]; fv[:, 6, F - 1] = (fu[:, 6, F - 1] + 1 + rng.integers(0, W - 1, N)) % W
    q[:, 7] = 0; q[1::2, 7] = 255
    st[:, :, 0] = 1
    return pack(v, q, k, fu, fv, st)
def setup_inputs_alike(rng):
    v, q, kid = letters(rng, False); fu, fv, st = front(rng, False)
    v[:] = v[:1].copy(); q[:] = q[:1].copy(); kid[:] = kid[:1].copy()
    for x in (fu, fv, st):
        for r in range(1, N):
            x[r, ::2] = x[0, ::2]; x[r, 1::2] = np.roll(x[0, 1::2], r * (F // N), axis=1)
    st[:, :, 0] = 1
    return pack(*mix(rng, v, q, kid, fu, fv), st)
def setup_inputs_spread(rng):
    v, q, kid = letters(rng, True); fu, fv, st = front(rng, True)
    return pack(*mix(rng, v, q, kid, fu, fv), st)
def check_inputs(d):
    bad = []
    for k, hi in (("vec", 255), ("mark", 255), ("kids", W - 1), ("fu", W - 1), ("fv", W - 1), ("fs", 1)):
        a = np.asarray(d[k]).astype(np.float32)
        if not np.all((a >= 0) & (a <= hi) & (a == np.floor(a))): bad.append("range of " + k)
    if not np.all(np.asarray(d["fs"])[:, :, 0] == 1): bad.append("first place of fs")
    return bad
def reference(vec, mark, kids, fu, fv, fs):
    vt = vec.astype(np.float32).astype(np.int64).reshape(N, 8, 16, W); qt = mark.astype(np.float32).astype(np.int64).reshape(N, 8, 16, W); kt = kids.astype(np.int64).reshape(N, 8, 16, W)
    u = np.stack([gentries(a) for a in fu]).astype(np.int64); v = np.stack([gentries(a) for a in fv]).astype(np.int64); st = fs.astype(np.int64)
    store = np.full((N, 8, 16, TS), -1, np.int64)
    for rnd in range(RO):
        a = pick(kt, u).transpose(0, 1, 3, 2).reshape(N, 8, 16 * F); b = pick(kt, v).transpose(0, 1, 3, 2).reshape(N, 8, 16 * F)
        d = np.add.accumulate(pick(vt, a) - pick(vt, b), axis=3)
        s0 = 16 * np.repeat(np.maximum.accumulate(np.where(st == 1, np.arange(F), 0), axis=2), 16, axis=2)
        d = d - np.where((s0 > 0)[:, :, None, :], pick(d, np.maximum(s0 - 1, 0)), 0)
        last = np.zeros((N, 8, F, 16), bool); last[:, :, F - 1, 15] = True; last[:, :, :F - 1, 15] = st[:, :, 1:] == 1
        cut = np.all(d == 0, axis=2) | last.reshape(N, 8, 16 * F)
        e = np.maximum(pick(qt, a), pick(qt, b)) + d; run = np.add.accumulate(e, axis=3)
        fac = {}
        for r in range(N):
            for g in range(8):
                t1 = np.flatnonzero(cut[r, g]); t0 = np.concatenate([np.zeros(1, np.int64), t1[:-1] + 1]); ln = t1 - t0 + 1
                c = np.flatnonzero((ln <= LM) & ~((ln == 1) & (a[r, g, t0] == b[r, g, t0])))[:FC]
                t0 = t0[c]; t1 = t1[c]; ln = ln[c]
                z = (run[r, g][:, t1] - run[r, g][:, t0] + e[r, g][:, t0]) & 255
                h = (WT @ z) & (N * TS - 1)
                fac[r, g] = (t0, ln, z, h & (N - 1), h >> LB, np.zeros(len(c), bool))
        for o in range(N):
            for g in range(8):
                ix = [np.flatnonzero(fac[r, g][3] == o)[:CAP] for r in range(N)]
                zz = np.concatenate([fac[r, g][2][:, ix[r]] for r in range(N)], axis=1); pp = np.concatenate([fac[r, g][4][ix[r]] for r in range(N)])
                i = np.flatnonzero(np.any(store[o, g][:, pp] != zz, axis=0))
                win = i[np.unique(pp[i], return_index=True)[1]]
                store[o, g][:, pp[win]] = zz[:, win]
                new = np.zeros(len(pp), bool); new[win] = True; n = 0
                for r in range(N):
                    fac[r, g][5][ix[r]] = new[n:n + len(ix[r])]; n += len(ix[r])
        u = np.zeros((N, 8, F), np.int64); v = np.zeros((N, 8, F), np.int64); st = np.ones((N, 8, F), np.int64)
        for r in range(N):
            for g in range(8):
                t0, ln, z, o, p, new = fac[r, g]
                n = np.flatnonzero(new); to = np.add.accumulate(ln[n]); n = n[to <= F]; j = 0
                for x in n:
                    L = int(ln[x]); t = int(t0[x])
                    u[r, g, j:j + L] = a[r, g, t:t + L]; v[r, g, j:j + L] = b[r, g, t:t + L]; st[r, g, j + 1:j + L] = 0; j += L
    return {"yt": store.reshape(N, 128, TS).astype(np.float32).astype(BF), "yu": u.astype(np.float32), "yv": v.astype(np.float32), "ys": st.astype(np.float32)}

@@ -1,0 +1,573 @@
+import math
+from concourse.bass import DstId, RemoteDMATransfer
+from concourse.mybir import AluOpType, AxisListType, ActivationFunctionType
+
+A = AluOpType
+AF = ActivationFunctionType
+W, F, FC, CAP, TS, RO = 3456, 256, 512, 64, 2048, 3
+P = 16 * F
+MAG = float(2 ** 27)
+RND = float(2 ** 23)
+CH = [(0, 512), (512, 512), (1024, 1024), (2048, 1024), (3072, 512), (3584, 512)]
+ORDER = "BABABABABABAABABABBBABBB"
+TW = 288
+SD = 2064
+SW = SD + 256
+
+
+def shapes(kind, dtype, text):
+    return {w.split(":")[0]: (kind, [128, int(w.split(":")[1])], dtype) for w in text.split()}
+
+
+SCRATCH = {}
+SCRATCH.update(shapes("sbuf", "int32", "KID:3456 FUI:32 FSI:256 ZI:512 Z8:512 HI:32 OW:32 HT:16 HP:16 HR:256 RI:256 CI:1280"))
+SCRATCH.update(shapes("sbuf", "uint16", "FUV:32 KU:512 OPU:16 JT:32 T1:32 OFF:32 PU:16 R1:256 SU:16 OF2:32 CT:16 EXL:16"))
+SCRATCH.update(shapes("sbuf", "bfloat16", "VEC:3456 MRK:3456 FSB:256 NF:264 LASTF:256 EQ:256 KH:576 KL:576 MF:4096 VV:4096 DF:4096 AB:4096 "
+                      "NS:4112 QV:4096 CU:264 CV:256 CB:256 CD:264 XL:256 L2B:8 JW:768 JK:512 OO:512 LL:512 ZB:512 OHB:132 "
+                      "STO:2320 NQ:256 ED:256 EO:1920 NK:512 NL:40 KB:32 H:256 M2:256 YH:512 YL:512 CM:4096 JR:256 "
+                      "SND:2304 ARR:768 NEW:768 RPL:2304"))
+SCRATCH.update(shapes("sbuf", "float32", "KF:512 D:4096 EM:4096 EE:4096 LG:256 XLI:256 SC:256 XC:256 T0:512 Z1:512 SN:132 RA:132 RB:132 R2:66 RQ:40 "
+                      "RM:256 UH:256 NXT:768 NFX:256 FM:256 PP:256 PQ:256 MD:256 OUTF:768 CF:1280 CR:1792 SM:800"))
+VIEW = {"MQ": ("DF", 0, 4096)}
+for _w in ("L2:16 LT:8 PN:16 OP1:16 OP2:16 OP3:16 LEN:32 INV:32 OV:32 D2:32 O1:32 O2:32 O3:32 O4:32 IV:16 PF:16 P1:16 PM1:16 S1:16 "
+           "S2:16 S3:16 NP:32 NP2:32 SF:32 ST:32 EN:32 PE1:32 X1:32 X2:32 KP:32 TOT:8").split():
+    _n, _k = _w.split(":")
+    VIEW[_n] = ("SM", sum(x[2] for x in VIEW.values() if x[0] == "SM"), int(_k))
+BANKS = ("BA", "BB", "BC", "BD", "BE", "BF", "BG", "BH")
+SCRATCH.update({b: ("psum", [128, 512], "float32") for b in BANKS})
+SEMAPHORES = ["qv", "qs", "qt", "qg"] + ["ld%d" % k for k in range(7)] + ["st%d" % k for k in range(4)] + \
+             ["%s%d" % (s, r) for s in ("ka", "ra", "lk", "lr") for r in range(RO)]
+
+
+def rank_program(g, core, T, topo):
+    me = T.rank_of(core)
+    if me is None:
+        return
+    cores = list(T.cores)
+    N = len(cores)
+
+    def masks(src):
+        s = cores[src]
+        out = [d for d in range(N) if d != src and topo.chip(cores[d]) != topo.chip(s)]
+        on = [d for d in range(N) if d != src and topo.chip(cores[d]) == topo.chip(s)]
+        res = {}
+        used = []
+        for ds in (out, on):
+            if ds:
+                lst = [e for e in topo.engines(s, cores[ds[0]]) if e not in used]
+                n = 1
+                while n * 2 * len(ds) <= len(lst):
+                    n *= 2
+                for x, d in enumerate(ds):
+                    res[d] = lst[x * n:(x + 1) * n]
+                    used = used + res[d]
+        return res
+
+    queues = {"v": g.vector, "s": g.scalar, "t": g.tensor, "g": g, "y": g.sync}
+    count = {}
+    known = {q: {} for q in queues}
+    waited = {}
+    recs = {}
+    finals = {}
+
+    def dowaits(q, reads, writes):
+        best = {}
+        for regs, wr in ((reads, False), (writes, True)):
+            for (b, lo, hi) in regs:
+                for rec in recs.get(b, []):
+                    if rec[0] < hi and lo < rec[1] and (wr or rec[2]):
+                        s, v = rec[3]
+                        if known[q].get(s, 0) < v and best.get(s, (0, None))[0] < v:
+                            best[s] = (v, rec[4])
+        for s in sorted(best, key=lambda s: -sum(best[s][1].values())):
+            v, clk = best[s]
+            if known[q].get(s, 0) >= v:
+                continue
+            queues[q].wait_ge(T.sem[s], v)
+            waited[s] = max(waited.get(s, 0), v)
+            known[q][s] = v
+            for a, b in clk.items():
+                known[q][a] = max(known[q].get(a, 0), b)
+
+    def note(q, tok, reads, writes):
+        clk = dict(known[q])
+        clk[tok[0]] = max(clk.get(tok[0], 0), tok[1])
+        for (b, lo, hi) in writes:
+            recs[b] = [r for r in recs.get(b, []) if not (lo <= r[0] and r[1] <= hi)] + [(lo, hi, True, tok, clk)]
+        for (b, lo, hi) in reads:
+            recs[b] = [r for r in recs.get(b, []) if not (r[0] == lo and r[1] == hi and not r[2] and r[3][0] == tok[0])] + [(lo, hi, False, tok, clk)]
+        finals[tok[0]] = max(finals.get(tok[0], 0), tok[1])
+
+    def bankfix(reads, writes):
+        w = [(x[0], 0, 512) if x[0] in BANKS else x for x in writes] + [(x[0], 0, 512) for x in reads if x[0] in BANKS]
+        return [x for x in reads if x[0] not in BANKS], w
+
+    def op(q, fn, reads, writes):
+        reads, writes = bankfix(reads, writes)
+        dowaits(q, reads, writes)
+        s = "q" + q
+        fn().then_inc(T.sem[s], 1)
+        count[s] = count.get(s, 0) + 1
+        note(q, (s, count[s]), reads, writes)
+
+    def dma(q, sem, out, in_):
+        dowaits(q, in_[1], out[1])
+        queues[q].dma_start(out=out[0], in_=in_[0]).then_inc(T.sem[sem], 16)
+        note(q, (sem, 16), in_[1], out[1])
+
+    def R(name, lo=None, hi=None, step=None, p=None):
+        if name in VIEW:
+            name, at, n = VIEW[name]
+            lo, hi = (at, at + n) if lo is None else (at + lo, at + hi)
+        t = T[name]
+        if lo is None:
+            lo, hi = 0, t.shape[1]
+        if p is not None:
+            ap = t[p[0]:p[1], lo:hi]
+        else:
+            ap = t[:, lo:hi] if step is None else t[:, lo:hi:step]
+        return (ap, [(name, lo, hi)])
+
+    def I(win, off):
+        return (win[0].indirect(off[0]), win[1] + off[1])
+
+    def rg(*xs):
+        return [r for x in xs if isinstance(x, tuple) for r in x[1]]
+
+    def va(x):
+        return x[0] if isinstance(x, tuple) else x
+
+    def copy(out, in_):
+        op("v", lambda: g.vector.tensor_copy(out=out[0], in_=in_[0]), rg(in_) + out[1][1:], out[1][:1])
+
+    def tt(out, a, b, o):
+        op("v", lambda: g.vector.tensor_tensor(out=out[0], in0=a[0], in1=b[0], op=o), rg(a, b), out[1])
+
+    def ts(out, a, s1, o1, s2=None, o2=None):
+        if o2 is None:
+            op("v", lambda: g.vector.tensor_scalar(out=out[0], in0=a[0], scalar1=va(s1), scalar2=None, op0=o1), rg(a, s1), out[1])
+        else:
+            op("v", lambda: g.vector.tensor_scalar(out=out[0], in0=a[0], scalar1=va(s1), scalar2=va(s2), op0=o1, op1=o2), rg(a, s1, s2), out[1])
+
+    def scan(out, d0, d1, init, o1, o2):
+        op("v", lambda: g.vector.tensor_tensor_scan(out=out[0], data0=d0[0], data1=d1[0], initial=va(init), op0=o1, op1=o2), rg(d0, d1, init), out[1])
+
+    def reduce(out, in_):
+        op("v", lambda: g.vector.tensor_reduce(out=out[0], in_=in_[0], axis=AxisListType.X, op=A.add), in_[1], out[1])
+
+    def fill(out, c):
+        op("v", lambda: g.vector.memset(out[0], c), [], out[1])
+
+    def act(out, in_, f, bias=0.0, scale=1.0):
+        op("s", lambda: g.scalar.activation(out=out[0], in_=in_[0], func=f, bias=bias, scale=scale), rg(in_), out[1])
+
+    def mm(out, prs):
+        rd, wr = bankfix(rg(*[x for p in prs for x in p[:2]]), out[1])
+        ins = None
+        for k, p in enumerate(prs):
+            dowaits("t", rg(p[0], p[1]), wr)
+            o = p[2] if len(p) > 2 else out
+            ins = g.tensor.matmul(out=o[0], lhsT=p[0][0], rhs=p[1][0], start=(k == 0), stop=(k == len(prs) - 1))
+        ins.then_inc(T.sem.qt, 1)
+        count["qt"] = count.get("qt", 0) + 1
+        note("t", ("qt", count["qt"]), rd, wr)
+
+    def iota(out, pat, base, cm, flag=False):
+        if flag:
+            op("g", lambda: g.iota(out[0], pat, base, cm, allow_small_or_imprecise_dtypes=True), [], out[1])
+        else:
+            op("g", lambda: g.iota(out[0], pat, base, cm), [], out[1])
+
+    def gfill(out, c):
+        iota(out, [[0, out[1][0][2] - out[1][0][1]]], c, 0, True)
+
+    dma("y", "ld0", R("FUI", 0, 16), (T.fu[:], []))
+    dma("s", "ld1", R("FUI", 16, 32), (T.fv[:], []))
+    dma("s", "ld2", R("FSI", 0, 256, p=(0, 8)), (T.fs[:], []))
+    g.sync.dma_start(out=T.KID[0:64, :], in_=T.kids[0:64, :]).then_inc(T.sem.ld3, 16)
+    g.scalar.dma_start(out=T.KID[64:128, :], in_=T.kids[64:128, :]).then_inc(T.sem.ld4, 16)
+    recs["KID"] = [(0, W, True, ("ld3", 16), {"ld3": 16}), (0, W, True, ("ld4", 16), {"ld4": 16})]
+    finals["ld3"] = finals["ld4"] = 16
+    dma("y", "ld5", R("VEC"), (T.vec[:], []))
+    dma("s", "ld6", R("MRK"), (T.mark[:], []))
+
+    free = {"CI": 0, "CF": 0, "CM": 0, "CR": 0}
+
+    def new(buf, n):
+        lo = free[buf]
+        free[buf] = lo + (n + 15) // 16 * 16
+        return R(buf, lo, lo + n)
+
+    def part(m, a, b):
+        return R(m[1][0][0], m[1][0][1] + a, m[1][0][1] + b)
+
+    def win(m, i):
+        return part(m, 15 - i, 143 - i)
+
+    pI = new("CI", 1); cI = new("CI", 144); ktI = new("CI", 32); kdI = new("CI", 16); ksI = new("CI", 16); aI = new("CI", 256); exI = new("CI", 16)
+    iota(pI, [[0, 1]], 0, 1)
+    iota(cI, [[1, 144]], 0, 0)
+    iota(ktI, [[16, 32]], 256, 0)
+    iota(kdI, [[1, 16]], 512, 0)
+    iota(ksI, [[16, 16]], SD, 0)
+    iota(aI, [[1, 256]], 0, 0)
+    iota(exI, [[1, 16]], 0, 0)
+    gfill(R("MF"), 1)
+    K1 = new("CR", 512); IQ = new("CR", 256)
+    iota(K1, [[1, 512]], -4096, 0, True)
+    iota(IQ, [[1, 256]], 0, 0, True)
+    iota(R("JR"), [[1, 16], [16, 16]], 0, 0, True)
+    gfill(R("STO"), -1)
+    gfill(R("SND", 0, 256), -1)
+    gfill(R("KH"), 0)
+    gfill(R("KL"), 0)
+    gfill(R("RPL", 256, 768), 0)
+    for r in range(1, RO):
+        gfill(R("SND", 768 * r, 768 * r + 256), -1)
+        gfill(R("RPL", 768 * r + 256, 768 * r + 768), 0)
+    pmI = new("CI", 1); pgI = new("CI", 1); cgI = new("CI", 144); cmI = new("CI", 144); amI = new("CI", 256)
+    ts(pmI, pI, 15, A.bitwise_and)
+    ts(pgI, pI, 4, A.arith_shift_right)
+    ts(cgI, cI, 4, A.arith_shift_right)
+    ts(cmI, cI, 15, A.bitwise_and)
+    PM = new("CF", 1); PG = new("CF", 1); CG = new("CF", 144); CMF = new("CF", 144); PX = new("CF", 1)
+    copy(PM, pmI); copy(PG, pgI); copy(CG, cgI); copy(CMF, cmI); copy(PX, pI)
+    BLK = new("CM", 144); C15 = new("CM", 144); MST = new("CM", 144); G8 = new("CM", 8); R8 = new("CM", 128)
+    ts(BLK, CG, PG, A.is_equal)
+    ts(C15, CMF, 15.0, A.is_equal)
+    tt(MST, BLK, C15, A.mult)
+    ts(G8, part(cI, 0, 8), PG, A.is_equal)
+    ts(R8, part(CG, 0, 128), PX, A.is_equal)
+    ts(R("FSB", 0, 256, p=(0, 8)), R("FSI", 0, 256, p=(0, 8)), -1.0, A.mult, 1.0, A.add)
+    r0 = R8[1][0][1]
+    mm(R("BA", 0, 256), [((T.CM[0:8, r0:r0 + 128], R8[1]), R("FSB", 0, 256, p=(0, 8)))])
+    fill(R("NF"), 0.0)
+    copy(R("NF", 0, 256), R("BA", 0, 256))
+    copy(R("FUV"), R("FUI"))
+    WC = new("CF", 1)
+    ts(WC, PM, -14.0, A.mult, 255.0, A.add)
+
+    def scaled(src, by, n=144):
+        m = new("CM", n)
+        ts(m, part(src, 0, n), by, A.mult)
+        return m
+    MSL = scaled(MST, -float(2 ** 36)); MS = scaled(MST, 0.0625); MSC = scaled(MST, 2.0 ** -8); MSW = scaled(MST, WC)
+    MS4 = scaled(MST, 4096.0); MSI = scaled(MST, PM)
+    BW = scaled(BLK, WC, 128); BN = scaled(BLK, -1.0, 128); BI = scaled(BLK, PM, 128); G8S = scaled(G8, 0.0625, 8)
+    B1 = part(BLK, 0, 128)
+    DK = new("CF", 128); TMP = new("CF", 128); TM2 = new("CF", 128); CM1 = part(CMF, 0, 128)
+    ts(DK, CM1, PM, A.subtract)
+
+    def masked(o, c):
+        m = new("CM", 128)
+        ts(TMP, DK, c, o)
+        tt(m, TMP, B1, A.mult)
+        return m
+    TRS = masked(A.is_gt, 0.0); TRI = masked(A.is_ge, 0.0); TGE = masked(A.is_le, 0.0); IDN = masked(A.is_equal, 0.0)
+    S0 = masked(A.is_equal, 1.0); S1 = masked(A.is_equal, -15.0)
+    TRN = new("CM", 128)
+    ts(TMP, IDN, 65.0, A.mult)
+    tt(TRN, TMP, TRI, A.subtract)
+    TRX = new("CM", 128)
+    ts(TMP, IDN, -4096.0, A.mult)
+    tt(TRX, TRS, TMP, A.add)
+    DA = new("CF", 128); DB = new("CF", 128)
+    R4 = new("CR", 128); R4P = new("CR", 128); C4 = new("CR", 1)
+    ts(DB, CM1, 0.0, A.is_equal)
+    ts(DA, CM1, 0.0, A.is_gt, 0.25, A.mult)
+    scan(R4, DA, DB, 0.0, A.mult, A.add)
+    ts(TMP, CM1, 0.0, A.is_gt, 4.0, A.mult)
+    scan(R4P, TMP, DB, 0.0, A.mult, A.add)
+    tt(TM2, IDN, R4P, A.mult)
+    reduce(C4, TM2)
+    A1 = new("CM", 128); A0 = new("CM", 128); A2 = new("CM", 128)
+    ts(TMP, R4, C4, A.mult, float(4 ** 16), A.mult)
+    tt(A1, TMP, B1, A.mult)
+    ts(TM2, TMP, float(4 ** 16), A.mult)
+    tt(A0, TM2, TRS, A.mult)
+    ts(TM2, TMP, float(4.0 ** -16), A.mult)
+    tt(A2, TM2, TGE, A.mult)
+    KT = new("CR", 32); KD = new("CR", 16); KS = new("CR", 16); PM16 = new("CF", 1); PM85 = new("CF", 1); ZR = new("CR", 256)
+    MK = new("CR", 256); RS = new("CR", 132)
+    ts(KT, ktI, PM, A.add)
+    ts(PM16, PM, 16.0, A.mult)
+    ts(KD, kdI, PM16, A.add)
+    ts(KS, ksI, PM, A.add)
+    ts(PM85, PM, 8.5, A.add)
+    ts(amI, aI, 15, A.bitwise_and)
+    ts(MK, amI, PM, A.is_le, 4096.0, A.mult)
+    ts(MK, MK, 1.0, A.add)
+    copy(R("EXL"), exI)
+    fill(ZR, 0.0)
+    fill(RS, 1.0)
+    for o in range(N):
+        fill(part(RS, 33 * o, 33 * o + 1), 0.0)
+    fill(R("OHB"), 0.0); fill(R("CD"), 0.0); fill(R("CU"), 0.0); fill(R("NL"), 0.0); fill(R("NS", 0, 16), 0.0)
+    ts(R("CU", 1, 2), PM, 15.0, A.is_equal)
+
+    def relay(outb, n, *parts):
+        mm(R(outb, 0, n), [(win(m, i), R(b, lo + i, lo + 16 * n, 16)) for m, b, lo in parts for i in range(16)])
+
+    def gv(c):
+        a, n = CH[c]
+        act(R("VV", a, a + n), I(R("VEC"), R("KU", 256 + a // 16, 256 + (a + n) // 16)), AF.Copy)
+
+    def gq(c):
+        a, n = CH[c]
+        act(R("QV", a, a + n), I(R("MRK"), R("KU", 256 + a // 16, 256 + (a + n) // 16)), AF.Copy)
+
+    def vphase():
+        copy(R("KU", 256, 512), I(R("KID"), R("FUV", 16, 32)))
+        copy(R("KU", 0, 256), I(R("KID"), R("FUV", 0, 16)))
+        gv(0)
+        gv(1)
+        copy(R("MF", 0, P, 16), R("NF", 0, 256))
+        ts(R("LASTF"), R("NF", 1, 257), -1.0, A.mult, 1.0, A.add)
+        copy(R("KF"), R("KU"))
+        for c, (a, n) in enumerate(CH):
+            tt(R("DF", a, a + n), I(R("VEC"), R("KU", a // 16, (a + n) // 16)), R("VV", a, a + n), A.subtract)
+            if c == 1:
+                tt(R("EQ"), R("KF", 0, 256), R("KF", 256, 512), A.is_equal)
+            scan(R("D", a, a + n), R("MF", a, a + n), R("DF", a, a + n), R("D", a - 1, a) if a else 0.0, A.mult, A.add)
+            if c + 2 < len(CH):
+                gv(c + 2)
+            elif c + 2 == len(CH):
+                gq(0)
+            act(R("AB", a, a + n), R("D", a, a + n), AF.Abs)
+            j0, j1 = a // 16, (a + n) // 16
+            mm(R("BC", j0, j1), [(win(MST, i), R("AB", a + i, a + n, 16)) for i in range(16)] + [(win(MSL, 15), R("LASTF", j0, j1))])
+
+    def comp():
+        ts(R("CU", 2, 258), R("BC", 0, 256), 0.0, A.is_le)
+        mm(R("BD", 0, 256), [(A0, R("CU", 2, 258)), (A1, R("CU", 1, 257)), (A2, R("CU", 0, 256))])
+        mm(R("BE", 0, 256), [(S0, R("CU", 2, 258)), (S1, R("CU", 1, 257))])
+        yield
+        tt(R("CV"), R("BD", 0, 256), R("CU", 2, 258), A.min)
+        act(R("LG"), R("BD", 0, 256), AF.Ln, 0.25)
+        act(R("XLI"), R("LG"), AF.Identity, 32.1 + RND, -1.0 / math.log(4.0))
+        tt(R("CB"), R("BE", 0, 256), R("EQ"), A.mult)
+        yield
+        tt(R("CD", 1, 257), R("CV"), R("CB"), A.is_gt)
+        mm(R("BH", 0, 16), [(win(MST, a), R("CD", 1 + 16 * a, 17 + 16 * a)) for a in range(16)])
+        mm(R("BF", 0, 256), [(TRX, R("CD", 1, 257))])
+        mm(R("BG", 0, 256), [(B1, R("CD", 0, 256))])
+        yield
+        scan(R("L2"), R("BH", 0, 16), part(ZR, 0, 16), 0.0, A.add, A.add)
+        ts(R("PN"), R("BH", 0, 16), 0.0, A.is_equal, 8192.0, A.mult)
+        copy(R("L2B", 0, 1), R("L2", 15, 16))
+        tt(R("OP1"), R("BH", 0, 16), R("PN"), A.subtract)
+        mm(R("BD", 0, 1), [(TRS, R("L2B", 0, 1))])
+        yield
+        tt(R("OP2"), R("L2"), R("OP1"), A.subtract)
+        copy(R("LT", 0, 1), R("BD", 0, 1))
+        gfill(R("JW", 0, 512), 0)
+        yield
+        ts(R("OP1"), R("OP2"), R("LT", 0, 1), A.add)
+        ts(R("OP2"), R("OP1"), 512.0, A.is_ge, 8192.0, A.mult)
+        tt(R("OP3"), R("OP1"), R("OP2"), A.max)
+        tt(R("OP1"), R("OP3"), KD, A.min)
+        copy(R("OPU"), R("OP1"))
+        copy(I(R("JW"), R("OPU")), R("JR"))
+        yield
+        scan(R("JK"), R("JW", 0, 512), R("JW", 0, 512), 0.0, A.max, A.max)
+        relay("BD", 32, (MS, "JK", 0))
+        scan(R("SC"), R("BG", 0, 256), ZR, 0.0, A.add, A.add)
+        yield
+        ts(R("XL"), R("XLI"), -RND, A.add)
+        copy(R("JT"), R("BD", 0, 32))
+        yield
+        tt(R("XC"), R("BF", 0, 256), R("SC"), A.add)
+        yield
+        tt(R("OO"), I(R("XC"), R("JT")), K1, A.is_equal)
+        tt(R("LL"), I(R("XL"), R("JT")), R("OO"), A.mult)
+        relay("BE", 32, (MST, "JK", 0), (MSI, "OO", 0))
+        relay("BF", 32, (MST, "LL", 0))
+        mm(R("BG", 0, 512), [(B1, R("JK")), (BI, R("OO")), (BN, R("LL"))])
+        yield
+        copy(R("T1"), R("BE", 0, 32))
+        copy(R("LEN"), R("BF", 0, 32))
+        ts(R("INV"), R("BF", 0, 32), 0.0, A.is_equal, 8.0, A.mult)
+        act(R("T0"), R("BG", 0, 512), AF.Identity, 9.5)
+        yield
+
+    def qphase():
+        for c in range(1, len(CH)):
+            gq(c)
+        banks = ("BA", "BB")
+        rc = 0
+        for c, (a, n) in enumerate(CH):
+            tt(R("MQ", a, a + n), I(R("MRK"), R("KU", a // 16, (a + n) // 16)), R("QV", a, a + n), A.max)
+            for _ in range(2 if c >= 2 else 0):
+                b = banks[rc % 2]
+                mm(R(b, 0, 512), [(B1, R("AB", 512 * rc, 512 * rc + 512))])
+                act(R("NS", 512 * rc + 1, 512 * rc + 513), R(b, 0, 512), AF.Sign)
+                rc += 1
+            yield
+        tt(R("NS", 0, P, 16), R("NS", 0, P, 16), R("NF", 0, 256), A.mult)
+        yield
+        for dst, src in (("EE", "D"), ("EM", "MQ")):
+            for a in range(0, P, 1024):
+                scan(R(dst, a, a + 1024), R("NS", a, a + 1024), R(src, a, a + 1024), R(dst, a - 1, a) if a else 0.0, A.mult, A.add)
+                yield
+
+    def fused(src, dst, lsem, rsem):
+        m = masks(me)
+        tr, rd, tot = [], [], 0
+        for d in range(N):
+            if d != me:
+                rid, pid = topo.addr(cores[d])[:2]
+                x = src(d)
+                rd += x[1]
+                tot += len(m[d])
+                tr.append(RemoteDMATransfer(dst_ids=[DstId(rid=rid, pnc=pid)], dma_engine_mask=sum(1 << e for e in m[d]), remote_sem=T.sem[rsem], src=x[0], dst=dst[0]))
+        dowaits("g", rd, [])
+        g.remote_dma_fused(tr, local_sem=T.sem[lsem])
+        note("g", (lsem, tot), rd, [])
+
+    def landed(sem, buf, base):
+        tot = sum(len(masks(s)[me]) for s in range(N) if s != me)
+        for s in range(N):
+            if s != me:
+                recs.setdefault(buf, []).append((base + CAP * s, base + CAP * (s + 1), True, (sem, tot), {sem: tot}))
+        finals[sem] = tot
+
+    def keys(r):
+        act(R("Z1"), I(R("EE"), R("T1")), AF.Copy)
+        tt(R("ZI"), I(R("EM"), R("T1")), R("Z1"), A.add)
+        ts(R("Z8"), R("ZI"), 255, A.bitwise_and)
+        copy(R("ZB"), R("Z8"))
+        relay("BD", 32, (MSW, "ZB", 0))
+        copy(R("HI"), R("BD", 0, 32))
+        ts(R("OW"), R("HI"), 3, A.bitwise_and)
+        tt(R("OV"), R("OW"), R("INV"), A.add)
+        for o in range(N):
+            ts(R("OHB", 33 * o + 1, 33 * o + 33), R("OV"), float(o), A.is_equal)
+        mm(R("BE", 0, 132), [(BN, R("OHB"))])
+        mm(R("BF", 0, 132), [(TRN, R("OHB"))])
+        ts(R("D2"), R("OV"), 64.0, A.mult, 64.0, A.add)
+        scan(R("SN"), RS, R("BE", 0, 132), 0.0, A.mult, A.add)
+        tt(R("RA", 1, 132), R("BF", 1, 132), R("SN", 0, 131), A.add)
+        tt(R("RB", 1, 132), R("RA", 1, 132), R("OHB", 1, 132), A.mult)
+        tt(R("R2", 1, 66), R("RB", 1, 66), R("RB", 67, 132), A.add)
+        tt(R("RQ", 1, 33), R("R2", 1, 33), R("R2", 34, 66), A.add)
+        ts(R("O1"), R("RQ", 1, 33), 0.0, A.is_le, 4096.0, A.mult)
+        tt(R("O2"), R("D2"), R("RQ", 1, 33), A.subtract)
+        tt(R("O3"), R("O2"), R("O1"), A.max)
+        tt(R("O4"), R("O3"), KT, A.min)
+        copy(R("OFF"), R("O4"))
+        b, c = 768 * r, 256 * r + CAP * me
+        copy(I(R("SND", b, b + 768), R("OFF")), R("ZB"))
+        fused(lambda d: R("SND", b + CAP * d, b + CAP * d + CAP), R("ARR", c, c + CAP), "lk%d" % r, "ka%d" % r)
+        act(R("ARR", c, c + CAP), R("SND", b + CAP * me, b + CAP * me + CAP), AF.Copy)
+        fill(R("NXT", 0, 256), 1.0)
+        for k in range(2):
+            ts(R("KH", TW * k, TW * k + 256), R("KU", 256 * k, 256 * k + 256), MAG, A.add, MAG, A.subtract)
+            tt(R("KL", TW * k, TW * k + 256), R("KF", 256 * k, 256 * k + 256), R("KH", TW * k, TW * k + 256), A.subtract)
+        landed("ka%d" % r, "ARR", 256 * r)
+
+    def owner(r):
+        b = 256 * r
+        arr = R("ARR", b, b + 256)
+        relay("BG", 16, (MSW, "ARR", b))
+        mm(R("BH", 0, 256), [(BW, arr)])
+        copy(R("HT"), R("BG", 0, 16))
+        ts(R("HP"), R("HT"), 2, A.arith_shift_right, TS - 1, A.bitwise_and)
+        ts(R("IV"), R("HT"), 0.0, A.is_lt, float(TS), A.mult)
+        tt(R("PF"), R("HP"), R("IV"), A.max)
+        copy(R("PU"), R("PF"))
+        tt(R("NQ"), I(R("STO"), R("PU")), arr, A.not_equal)
+        relay("BD", 16, (MS4, "NQ", 0))
+        mm(R("BE", 0, 256), [(B1, R("NQ"))])
+        copy(R("HR"), R("BH", 0, 256))
+        ts(R("RI"), R("HR"), 2, A.arith_shift_right, TS - 1, A.bitwise_and)
+        ts(R("R1"), R("RI"), 1.0, A.add)
+        tt(R("RM"), R("RI"), MK, A.add)
+        ts(R("P1"), R("PF"), 1.0, A.add)
+        tt(R("PM1"), R("BD", 0, 16), R("P1"), A.min)
+        tt(R("ED"), I(R("PM1"), R("EXL")), R("RM"), A.is_equal)
+        eo = [(B1, R("ED"))]
+        lo = 0
+        for m in range(15):
+            n = 240 - 16 * m
+            ts(R("EO", lo, lo + n), R("R1", 16 * m + 16, 256), R("PM1", m, m + 1), A.is_equal)
+            eo.append((B1, R("EO", lo, lo + n), R("BF", 16 * m + 16, 256)))
+            lo += n
+        ts(R("UH"), R("BE", 0, 256), 1.0, A.min, 0.5, A.mult)
+        mm(R("BF", 0, 256), eo)
+        tt(R("NEW", b, b + 256), R("UH"), R("BF", 0, 256), A.is_gt)
+        rb = 768 * r + CAP * me
+        fused(lambda d: R("NEW", b + CAP * d, b + CAP * d + CAP), R("RPL", rb, rb + CAP), "lr%d" % r, "ra%d" % r)
+        act(R("RPL", rb, rb + CAP), R("NEW", b + CAP * me, b + CAP * me + CAP), AF.Copy)
+        landed("ra%d" % r, "RPL", 768 * r)
+        relay("BG", 16, (MS, "NEW", b))
+        ts(R("S1"), R("BG", 0, 16), 0.0, A.is_equal, 8192.0, A.mult)
+        tt(R("S2"), R("S1"), R("PF"), A.max)
+        tt(R("S3"), R("S2"), KS, A.min)
+        copy(R("SU"), R("S3"))
+        copy(I(R("STO"), R("SU")), arr)
+        if r == RO - 1:
+            dma("y", "st0", (T.yt[:], []), R("STO", 0, TS))
+
+    def nextfront(r):
+        b = 768 * r
+        copy(R("NK"), I(R("RPL", b, b + 768), R("OFF")))
+        relay("BH", 32, (MS, "NK", 0))
+        tt(R("NL", 1, 33), R("BH", 0, 32), R("LEN"), A.mult)
+        mm(R("BD", 0, 32), [(B1, R("NL", 0, 32))])
+        mm(R("BE", 0, 32), [(TRS, R("NL", 1, 33))])
+        ts(R("NP"), R("NL", 1, 33), 0.0, A.is_equal, 2048.0, A.mult)
+        scan(R("SF"), R("BD", 0, 32), part(ZR, 0, 32), 0.0, A.add, A.add)
+        tt(R("NP2"), R("NP"), R("NL", 1, 33), A.add)
+        tt(R("ST"), R("BE", 0, 32), R("SF"), A.add)
+        tt(R("EN"), R("ST"), R("NP2"), A.add)
+        ts(R("PE1"), R("EN"), 256.0, A.is_gt, 32768.0, A.mult)
+        ts(R("KP"), R("EN"), 256.0, A.is_le)
+        tt(R("X1"), R("ST"), R("PE1"), A.max)
+        tt(R("KB"), R("KP"), R("NL", 1, 33), A.mult)
+        tt(R("X2"), R("X1"), KT, A.min)
+        mm(R("BC", 0, 32), [(B1, R("KB"))])
+        copy(R("OF2"), R("X2"))
+        copy(I(R("NXT"), R("OF2")), R("T0"))
+        ts(R("NFX"), R("NXT", 0, 256), 1.0, A.is_equal)
+        scan(R("PP"), R("NFX"), R("NXT", 0, 256), 0.0, A.mult, A.add)
+        ts(R("H"), R("PP"), MAG, A.add, MAG + 16.0, A.subtract)
+        relay("BF", 16, (MSC, "H", 0))
+        reduce(R("TOT", 0, 1), R("BC", 0, 32))
+        ts(R("FM"), IQ, R("TOT", 0, 1), A.is_ge, 16384.0, A.mult)
+        tt(R("PQ"), R("PP"), R("FM"), A.max)
+        tt(R("MD"), R("PQ"), R("H"), A.subtract)
+        ts(R("M2"), R("MD"), PM85, A.is_equal)
+        copy(R("CT"), R("BF", 0, 16))
+        for y, k0 in (("YH", "KH"), ("YL", "KL")):
+            for k in range(2):
+                tt(R(y, 256 * k, 256 * k + 256), I(R(k0, TW * k, TW * k + TW), R("CT")), R("M2"), A.mult)
+        if r < RO - 1:
+            relay("BG", 32, (MST, "YH", 0), (MST, "YL", 0))
+        else:
+            mm((T.BG[0:8, 0:512], [("BG", 0, 512)]), [(G8, R("YH")), (G8, R("YL"))])
+        ts(R("FM"), IQ, R("TOT", 0, 1), A.is_lt)
+        tt(R("NF", 0, 256), R("FM"), R("NFX"), A.mult)
+        if r < RO - 1:
+            copy(R("FUV"), R("BG", 0, 32))
+        else:
+            mm((T.BH[0:8, 0:256], [("BH", 0, 512)]), [(G8S, R("NF", 0, 256))])
+            copy(R("OUTF", 0, 512, p=(0, 8)), (T.BG[0:8, 0:512], [("BG", 0, 512)]))
+            dma("y", "st1", (T.yu[:], []), R("OUTF", 0, 256, p=(0, 8)))
+            dma("s", "st2", (T.yv[:], []), R("OUTF", 256, 512, p=(0, 8)))
+            ts(R("OUTF", 512, 768, p=(0, 8)), (T.BH[0:8, 0:256], [("BH", 0, 512)]), -1.0, A.mult, 1.0, A.add)
+            dma("s", "st3", (T.ys[:], []), R("OUTF", 512, 768, p=(0, 8)))
+
+    for r in range(RO):
+        vphase()
+        two = {"B": qphase(), "A": comp()}
+        for x in ORDER:
+            next(two[x], None)
+        for x in two.values():
+            for _ in x:
+                pass
+        keys(r)
+        owner(r)
+        nextfront(r)
+    for s in sorted(finals):
+        if waited.get(s, 0) < finals[s]:
+            g.wait_ge(T.sem[s], finals[s])

@@ -9,7 +9,7 @@ P = 16 * F
 MAG = float(2 ** 27)
 RND = float(2 ** 23)
 CH = [(0, 512), (512, 512), (1024, 1024), (2048, 1024), (3072, 512), (3584, 512)]
-ORDER = "BABABABABABAABABABBBABBB"
+ORDER = "BABABABABABAAAAABBBABB"
 TW = 288
 SD = 2064
 SW = SD + 256
@@ -23,19 +23,19 @@ SCRATCH = {}
 SCRATCH.update(shapes("sbuf", "int32", "KID:3456 FUI:32 FSI:256 ZI:512 Z8:512 HI:32 OW:32 HT:16 HP:16 HR:256 RI:256 CI:1280"))
 SCRATCH.update(shapes("sbuf", "uint16", "FUV:32 KU:512 OPU:16 JT:32 T1:32 OFF:32 PU:16 R1:256 SU:16 OF2:32 CT:16 EXL:16"))
 SCRATCH.update(shapes("sbuf", "bfloat16", "VEC:3456 MRK:3456 FSB:256 NF:264 LASTF:256 EQ:256 KH:576 KL:576 MF:4096 VV:4096 DF:4096 AB:4096 "
-                      "NS:4112 QV:4096 CU:264 CV:256 CB:256 CD:264 XL:256 L2B:8 JW:768 JK:512 OO:512 LL:512 ZB:512 OHB:132 "
+                      "NS:4112 QV:4096 MQ:4096 CU:264 CV:256 CB:256 CD:264 XL:256 L2B:8 JW:768 JK:512 OO:512 LL:512 ZB:512 OHB:132 "
                       "STO:2320 NQ:256 ED:256 EO:1920 NK:512 NL:40 KB:32 H:256 M2:256 YH:512 YL:512 CM:4096 JR:256 "
                       "SND:2304 ARR:768 NEW:768 RPL:2304"))
-SCRATCH.update(shapes("sbuf", "float32", "KF:512 D:4096 EM:4096 EE:4096 LG:256 XLI:256 SC:256 XC:256 T0:512 Z1:512 SN:132 RA:132 RB:132 R2:66 RQ:40 "
+SCRATCH.update(shapes("sbuf", "float32", "KF:512 D:4096 EM:4096 LG:256 XLI:256 SC:256 XC:256 T0:512 SN:132 RA:132 RB:132 R2:66 RQ:40 "
                       "RM:256 UH:256 NXT:768 NFX:256 FM:256 PP:256 PQ:256 MD:256 OUTF:768 CF:1280 CR:1792 SM:800"))
-VIEW = {"MQ": ("DF", 0, 4096)}
+VIEW = {}
 for _w in ("L2:16 LT:8 PN:16 OP1:16 OP2:16 OP3:16 LEN:32 INV:32 OV:32 D2:32 O1:32 O2:32 O3:32 O4:32 IV:16 PF:16 P1:16 PM1:16 S1:16 "
            "S2:16 S3:16 NP:32 NP2:32 SF:32 ST:32 EN:32 PE1:32 X1:32 X2:32 KP:32 TOT:8").split():
     _n, _k = _w.split(":")
-    VIEW[_n] = ("SM", sum(x[2] for x in VIEW.values() if x[0] == "SM"), int(_k))
+    VIEW[_n] = ("SM", sum(x[2] for x in VIEW.values()), int(_k))
 BANKS = ("BA", "BB", "BC", "BD", "BE", "BF", "BG", "BH")
 SCRATCH.update({b: ("psum", [128, 512], "float32") for b in BANKS})
-SEMAPHORES = ["qv", "qs", "qt", "qg"] + ["ld%d" % k for k in range(7)] + ["st%d" % k for k in range(4)] + \
+SEMAPHORES = ["qv", "qs", "qt", "qg"] + ["ld%d" % k for k in range(9)] + ["st%d" % k for k in range(4)] + ["ac%d" % k for k in range(len(CH))] + \
              ["%s%d" % (s, r) for s in ("ka", "ra", "lk", "lr") for r in range(RO)]
 
 
@@ -115,6 +115,12 @@ def rank_program(g, core, T, topo):
         queues[q].dma_start(out=out[0], in_=in_[0]).then_inc(T.sem[sem], 16)
         note(q, (sem, 16), in_[1], out[1])
 
+    def addto(out, in_, sem):
+        dowaits("g", in_[1], out[1])
+        g.dma_start(out=out[0], in_=in_[0], accum_op=A.add).then_inc(T.sem[sem], 16)
+        count[sem] = count.get(sem, 0) + 16
+        note("g", (sem, count[sem]), in_[1], out[1])
+
     def R(name, lo=None, hi=None, step=None, p=None):
         if name in VIEW:
             name, at, n = VIEW[name]
@@ -184,12 +190,12 @@ def rank_program(g, core, T, topo):
     dma("y", "ld0", R("FUI", 0, 16), (T.fu[:], []))
     dma("s", "ld1", R("FUI", 16, 32), (T.fv[:], []))
     dma("s", "ld2", R("FSI", 0, 256, p=(0, 8)), (T.fs[:], []))
-    g.sync.dma_start(out=T.KID[0:64, :], in_=T.kids[0:64, :]).then_inc(T.sem.ld3, 16)
-    g.scalar.dma_start(out=T.KID[64:128, :], in_=T.kids[64:128, :]).then_inc(T.sem.ld4, 16)
-    recs["KID"] = [(0, W, True, ("ld3", 16), {"ld3": 16}), (0, W, True, ("ld4", 16), {"ld4": 16})]
-    finals["ld3"] = finals["ld4"] = 16
-    dma("y", "ld5", R("VEC"), (T.vec[:], []))
-    dma("s", "ld6", R("MRK"), (T.mark[:], []))
+    for k, (b, x) in enumerate((("KID", T.kids), ("VEC", T.vec), ("MRK", T.mark))):
+        s0, s1 = "ld%d" % (3 + 2 * k), "ld%d" % (4 + 2 * k)
+        g.sync.dma_start(out=T[b][0:64, :], in_=x[0:64, :]).then_inc(T.sem[s0], 16)
+        g.scalar.dma_start(out=T[b][64:128, :], in_=x[64:128, :]).then_inc(T.sem[s1], 16)
+        recs[b] = [(0, W, True, (s0, 16), {s0: 16}), (0, W, True, (s1, 16), {s1: 16})]
+        finals[s0] = finals[s1] = 16
 
     free = {"CI": 0, "CF": 0, "CM": 0, "CR": 0}
 
@@ -321,6 +327,7 @@ def rank_program(g, core, T, topo):
         copy(R("KU", 0, 256), I(R("KID"), R("FUV", 0, 16)))
         gv(0)
         gv(1)
+        gfill(R("JW", 0, 512), 0)
         copy(R("MF", 0, P, 16), R("NF", 0, 256))
         ts(R("LASTF"), R("NF", 1, 257), -1.0, A.mult, 1.0, A.add)
         copy(R("KF"), R("KU"))
@@ -360,7 +367,6 @@ def rank_program(g, core, T, topo):
         yield
         tt(R("OP2"), R("L2"), R("OP1"), A.subtract)
         copy(R("LT", 0, 1), R("BD", 0, 1))
-        gfill(R("JW", 0, 512), 0)
         yield
         ts(R("OP1"), R("OP2"), R("LT", 0, 1), A.add)
         ts(R("OP2"), R("OP1"), 512.0, A.is_ge, 8192.0, A.mult)
@@ -397,6 +403,7 @@ def rank_program(g, core, T, topo):
         rc = 0
         for c, (a, n) in enumerate(CH):
             tt(R("MQ", a, a + n), I(R("MRK"), R("KU", a // 16, (a + n) // 16)), R("QV", a, a + n), A.max)
+            addto(R("D", a, a + n), R("MQ", a, a + n), "ac%d" % c)
             for _ in range(2 if c >= 2 else 0):
                 b = banks[rc % 2]
                 mm(R(b, 0, 512), [(B1, R("AB", 512 * rc, 512 * rc + 512))])
@@ -405,10 +412,9 @@ def rank_program(g, core, T, topo):
             yield
         tt(R("NS", 0, P, 16), R("NS", 0, P, 16), R("NF", 0, 256), A.mult)
         yield
-        for dst, src in (("EE", "D"), ("EM", "MQ")):
-            for a in range(0, P, 1024):
-                scan(R(dst, a, a + 1024), R("NS", a, a + 1024), R(src, a, a + 1024), R(dst, a - 1, a) if a else 0.0, A.mult, A.add)
-                yield
+        for a in range(0, P, 1024):
+            scan(R("EM", a, a + 1024), R("NS", a, a + 1024), R("D", a, a + 1024), R("EM", a - 1, a) if a else 0.0, A.mult, A.add)
+            yield
 
     def fused(src, dst, lsem, rsem):
         m = masks(me)
@@ -432,8 +438,7 @@ def rank_program(g, core, T, topo):
         finals[sem] = tot
 
     def keys(r):
-        act(R("Z1"), I(R("EE"), R("T1")), AF.Copy)
-        tt(R("ZI"), I(R("EM"), R("T1")), R("Z1"), A.add)
+        copy(R("ZI"), I(R("EM"), R("T1")))
         ts(R("Z8"), R("ZI"), 255, A.bitwise_and)
         copy(R("ZB"), R("Z8"))
         relay("BD", 32, (MSW, "ZB", 0))

@@ -9,7 +9,7 @@ P = 16 * F
 MAG = float(2 ** 27)
 RND = float(2 ** 23)
 CH = [(0, 512), (512, 512), (1024, 1024), (2048, 1024), (3072, 512), (3584, 512)]
-ORDER = "BABABABABABAAAAABBBABB"
+ORDER = "BABABABABABAABAAABAB"
 TW = 288
 SD = 2064
 SW = SD + 256
@@ -27,10 +27,10 @@ SCRATCH.update(shapes("sbuf", "bfloat16", "VEC:3456 MRK:3456 FSB:256 NF:264 LAST
                       "STO:2320 NQ:256 ED:256 EO:1920 NK:512 NL:40 KB:32 H:256 M2:256 YH:512 YL:512 CM:4096 JR:256 "
                       "SND:2304 ARR:768 NEW:768 RPL:2304"))
 SCRATCH.update(shapes("sbuf", "float32", "KF:512 D:4096 EM:4096 LG:256 XLI:256 SC:256 XC:256 T0:512 SN:132 RA:132 RB:132 R2:66 RQ:40 "
-                      "RM:256 UH:256 NXT:768 NFX:256 FM:256 PP:256 PQ:256 MD:256 OUTF:768 CF:1280 CR:1792 SM:800"))
+                      "RM:256 UH:256 NXT:768 NFX:256 FM:256 FL:256 PP:256 MD:256 OUTF:768 CF:1280 CR:1792 SM:976"))
 VIEW = {}
 for _w in ("L2:16 LT:8 PN:16 OP1:16 OP2:16 OP3:16 LEN:32 INV:32 OV:32 D2:32 O1:32 O2:32 O3:32 O4:32 IV:16 PF:16 P1:16 PM1:16 S1:16 "
-           "S2:16 S3:16 NP:32 NP2:32 SF:32 ST:32 EN:32 PE1:32 X1:32 X2:32 KP:32 TOT:8").split():
+           "S2:16 S3:16 NP:32 NP2:32 SF:32 ST:32 EN:32 PE1:32 X1:32 X2:32 KP:32 W0:32 VT:32 TOT:8 TOB:8 X3:32").split():
     _n, _k = _w.split(":")
     VIEW[_n] = ("SM", sum(x[2] for x in VIEW.values()), int(_k))
 BANKS = ("BA", "BB", "BC", "BD", "BE", "BF", "BG", "BH")
@@ -165,7 +165,7 @@ def rank_program(g, core, T, topo):
         op("v", lambda: g.vector.memset(out[0], c), [], out[1])
 
     def act(out, in_, f, bias=0.0, scale=1.0):
-        op("s", lambda: g.scalar.activation(out=out[0], in_=in_[0], func=f, bias=bias, scale=scale), rg(in_), out[1])
+        op("s", lambda: g.scalar.activation(out=out[0], in_=in_[0], func=f, bias=va(bias), scale=va(scale)), rg(in_, bias, scale), out[1])
 
     def mm(out, prs):
         rd, wr = bankfix(rg(*[x for p in prs for x in p[:2]]), out[1])
@@ -255,7 +255,7 @@ def rank_program(g, core, T, topo):
 
     def scaled(src, by, n=144):
         m = new("CM", n)
-        ts(m, part(src, 0, n), by, A.mult)
+        act(m, part(src, 0, n), AF.Identity, 0.0, by)
         return m
     MSL = scaled(MST, -float(2 ** 36)); MS = scaled(MST, 0.0625); MSC = scaled(MST, 2.0 ** -8); MSW = scaled(MST, WC)
     MS4 = scaled(MST, 4096.0); MSI = scaled(MST, PM)
@@ -294,8 +294,9 @@ def rank_program(g, core, T, topo):
     ts(TM2, TMP, float(4.0 ** -16), A.mult)
     tt(A2, TM2, TGE, A.mult)
     KT = new("CR", 32); KD = new("CR", 16); KS = new("CR", 16); PM16 = new("CF", 1); PM85 = new("CF", 1); ZR = new("CR", 256)
-    MK = new("CR", 256); RS = new("CR", 132)
+    MK = new("CR", 256); RS = new("CR", 132); QT = new("CR", 16)
     ts(KT, ktI, PM, A.add)
+    ts(QT, part(KT, 0, 16), -256.0, A.add)
     ts(PM16, PM, 16.0, A.mult)
     ts(KD, kdI, PM16, A.add)
     ts(KS, ksI, PM, A.add)
@@ -327,14 +328,11 @@ def rank_program(g, core, T, topo):
         copy(R("KU", 0, 256), I(R("KID"), R("FUV", 0, 16)))
         gv(0)
         gv(1)
+        act(R("LASTF"), R("NF", 1, 257), AF.Identity, 1.0, -1.0)
         gfill(R("JW", 0, 512), 0)
         copy(R("MF", 0, P, 16), R("NF", 0, 256))
-        ts(R("LASTF"), R("NF", 1, 257), -1.0, A.mult, 1.0, A.add)
-        copy(R("KF"), R("KU"))
         for c, (a, n) in enumerate(CH):
             tt(R("DF", a, a + n), I(R("VEC"), R("KU", a // 16, (a + n) // 16)), R("VV", a, a + n), A.subtract)
-            if c == 1:
-                tt(R("EQ"), R("KF", 0, 256), R("KF", 256, 512), A.is_equal)
             scan(R("D", a, a + n), R("MF", a, a + n), R("DF", a, a + n), R("D", a - 1, a) if a else 0.0, A.mult, A.add)
             if c + 2 < len(CH):
                 gv(c + 2)
@@ -345,6 +343,8 @@ def rank_program(g, core, T, topo):
             mm(R("BC", j0, j1), [(win(MST, i), R("AB", a + i, a + n, 16)) for i in range(16)] + [(win(MSL, 15), R("LASTF", j0, j1))])
 
     def comp():
+        copy(R("KF", 256, 512), R("KU", 256, 512))
+        tt(R("EQ"), I(R("KID"), R("FUV", 0, 16)), R("KF", 256, 512), A.is_equal)
         ts(R("CU", 2, 258), R("BC", 0, 256), 0.0, A.is_le)
         mm(R("BD", 0, 256), [(A0, R("CU", 2, 258)), (A1, R("CU", 1, 257)), (A2, R("CU", 0, 256))])
         mm(R("BE", 0, 256), [(S0, R("CU", 2, 258)), (S1, R("CU", 1, 257))])
@@ -379,7 +379,7 @@ def rank_program(g, core, T, topo):
         relay("BD", 32, (MS, "JK", 0))
         scan(R("SC"), R("BG", 0, 256), ZR, 0.0, A.add, A.add)
         yield
-        ts(R("XL"), R("XLI"), -RND, A.add)
+        act(R("XL"), R("XLI"), AF.Identity, -RND)
         copy(R("JT"), R("BD", 0, 32))
         yield
         tt(R("XC"), R("BF", 0, 256), R("SC"), A.add)
@@ -399,21 +399,21 @@ def rank_program(g, core, T, topo):
     def qphase():
         for c in range(1, len(CH)):
             gq(c)
-        banks = ("BA", "BB")
+        banks = ("BA", "BB", "BC")
         rc = 0
         for c, (a, n) in enumerate(CH):
             tt(R("MQ", a, a + n), I(R("MRK"), R("KU", a // 16, (a + n) // 16)), R("QV", a, a + n), A.max)
             addto(R("D", a, a + n), R("MQ", a, a + n), "ac%d" % c)
             for _ in range(2 if c >= 2 else 0):
-                b = banks[rc % 2]
+                b = banks[rc % 3]
                 mm(R(b, 0, 512), [(B1, R("AB", 512 * rc, 512 * rc + 512))])
                 act(R("NS", 512 * rc + 1, 512 * rc + 513), R(b, 0, 512), AF.Sign)
                 rc += 1
             yield
         tt(R("NS", 0, P, 16), R("NS", 0, P, 16), R("NF", 0, 256), A.mult)
         yield
-        for a in range(0, P, 1024):
-            scan(R("EM", a, a + 1024), R("NS", a, a + 1024), R("D", a, a + 1024), R("EM", a - 1, a) if a else 0.0, A.mult, A.add)
+        for a in range(0, P, 2048):
+            scan(R("EM", a, a + 2048), R("NS", a, a + 2048), R("D", a, a + 2048), R("EM", a - 1, a) if a else 0.0, A.mult, A.add)
             yield
 
     def fused(src, dst, lsem, rsem):
@@ -465,6 +465,7 @@ def rank_program(g, core, T, topo):
         fused(lambda d: R("SND", b + CAP * d, b + CAP * d + CAP), R("ARR", c, c + CAP), "lk%d" % r, "ka%d" % r)
         act(R("ARR", c, c + CAP), R("SND", b + CAP * me, b + CAP * me + CAP), AF.Copy)
         fill(R("NXT", 0, 256), 1.0)
+        copy(R("KF", 0, 256), R("KU", 0, 256))
         for k in range(2):
             ts(R("KH", TW * k, TW * k + 256), R("KU", 256 * k, 256 * k + 256), MAG, A.add, MAG, A.subtract)
             tt(R("KL", TW * k, TW * k + 256), R("KF", 256 * k, 256 * k + 256), R("KH", TW * k, TW * k + 256), A.subtract)
@@ -473,8 +474,10 @@ def rank_program(g, core, T, topo):
     def owner(r):
         b = 256 * r
         arr = R("ARR", b, b + 256)
-        relay("BG", 16, (MSW, "ARR", b))
         mm(R("BH", 0, 256), [(BW, arr)])
+        relay("BG", 16, (MSW, "ARR", b))
+        copy(R("HR"), R("BH", 0, 256))
+        ts(R("RI"), R("HR"), 2, A.arith_shift_right, TS - 1, A.bitwise_and)
         copy(R("HT"), R("BG", 0, 16))
         ts(R("HP"), R("HT"), 2, A.arith_shift_right, TS - 1, A.bitwise_and)
         ts(R("IV"), R("HT"), 0.0, A.is_lt, float(TS), A.mult)
@@ -483,8 +486,6 @@ def rank_program(g, core, T, topo):
         tt(R("NQ"), I(R("STO"), R("PU")), arr, A.not_equal)
         relay("BD", 16, (MS4, "NQ", 0))
         mm(R("BE", 0, 256), [(B1, R("NQ"))])
-        copy(R("HR"), R("BH", 0, 256))
-        ts(R("RI"), R("HR"), 2, A.arith_shift_right, TS - 1, A.bitwise_and)
         ts(R("R1"), R("RI"), 1.0, A.add)
         tt(R("RM"), R("RI"), MK, A.add)
         ts(R("P1"), R("PF"), 1.0, A.add)
@@ -515,7 +516,9 @@ def rank_program(g, core, T, topo):
 
     def nextfront(r):
         b = 768 * r
-        copy(R("NK"), I(R("RPL", b, b + 768), R("OFF")))
+        last = r == RO - 1
+        act(R("NK", 0, 224), I(R("RPL", b, b + 768), part(R("OFF"), 0, 14)), AF.Copy)
+        copy(R("NK", 224, 512), I(R("RPL", b, b + 768), part(R("OFF"), 14, 32)))
         relay("BH", 32, (MS, "NK", 0))
         tt(R("NL", 1, 33), R("BH", 0, 32), R("LEN"), A.mult)
         mm(R("BD", 0, 32), [(B1, R("NL", 0, 32))])
@@ -532,28 +535,38 @@ def rank_program(g, core, T, topo):
         tt(R("X2"), R("X1"), KT, A.min)
         mm(R("BC", 0, 32), [(B1, R("KB"))])
         copy(R("OF2"), R("X2"))
+        op("s", lambda: g.scalar.activation(out=R("X3")[0], in_=T.BC[:, 0:32], func=AF.Copy, accum_out=R("TOT", 0, 1)[0]),
+           [("BC", 0, 32)], R("X3")[1] + R("TOT", 0, 1)[1])
+        if not last:
+            act(R("TOB", 0, 1), R("TOT", 0, 1), AF.Identity, 0.5, -1.0)
+            for k in range(2):
+                act(R("VT", 16 * k, 16 * k + 16), QT, AF.Sign, R("TOB", 0, 1))
+            act(R("VT"), R("VT"), AF.Relu, 0.0, -1.0)
+        else:
+            act(R("TOB", 0, 1), R("TOT", 0, 1), AF.Identity, 16384.0, -32768.0)
+            act(R("FM"), IQ, AF.Relu, R("TOB", 0, 1), 32768.0)
         copy(I(R("NXT"), R("OF2")), R("T0"))
         ts(R("NFX"), R("NXT", 0, 256), 1.0, A.is_equal)
         scan(R("PP"), R("NFX"), R("NXT", 0, 256), 0.0, A.mult, A.add)
         ts(R("H"), R("PP"), MAG, A.add, MAG + 16.0, A.subtract)
         relay("BF", 16, (MSC, "H", 0))
-        reduce(R("TOT", 0, 1), R("BC", 0, 32))
-        ts(R("FM"), IQ, R("TOT", 0, 1), A.is_ge, 16384.0, A.mult)
-        tt(R("PQ"), R("PP"), R("FM"), A.max)
-        tt(R("MD"), R("PQ"), R("H"), A.subtract)
+        if last:
+            tt(R("PP"), R("PP"), R("FM"), A.max)
+        tt(R("MD"), R("PP"), R("H"), A.subtract)
         ts(R("M2"), R("MD"), PM85, A.is_equal)
         copy(R("CT"), R("BF", 0, 16))
         for y, k0 in (("YH", "KH"), ("YL", "KL")):
             for k in range(2):
                 tt(R(y, 256 * k, 256 * k + 256), I(R(k0, TW * k, TW * k + TW), R("CT")), R("M2"), A.mult)
-        if r < RO - 1:
+        if not last:
             relay("BG", 32, (MST, "YH", 0), (MST, "YL", 0))
         else:
             mm((T.BG[0:8, 0:512], [("BG", 0, 512)]), [(G8, R("YH")), (G8, R("YL"))])
-        ts(R("FM"), IQ, R("TOT", 0, 1), A.is_lt)
-        tt(R("NF", 0, 256), R("FM"), R("NFX"), A.mult)
-        if r < RO - 1:
-            copy(R("FUV"), R("BG", 0, 32))
+        ts(R("FL"), IQ, R("TOT", 0, 1), A.is_lt)
+        tt(R("NF", 0, 256), R("FL"), R("NFX"), A.mult)
+        if not last:
+            tt(R("W0"), R("BG", 0, 32), R("VT"), A.mult)
+            copy(R("FUV"), R("W0"))
         else:
             mm((T.BH[0:8, 0:256], [("BH", 0, 512)]), [(G8S, R("NF", 0, 256))])
             copy(R("OUTF", 0, 512, p=(0, 8)), (T.BG[0:8, 0:512], [("BG", 0, 512)]))

import math
from concourse.bass import DstId, RemoteDMATransfer
from concourse.mybir import AluOpType, AxisListType, ActivationFunctionType

A = AluOpType
AF = ActivationFunctionType
W, F, FC, CAP, TS, RO = 3456, 256, 512, 64, 2048, 3
P = 16 * F
MAG = float(2 ** 27)
RND = float(2 ** 23)
CH = [(0, 512), (512, 512), (1024, 1024), (2048, 1024), (3072, 512), (3584, 512)]
ORDER = "BABABABABABAABAAABAB"
TW = 288
SD = 2064
SW = SD + 256


def shapes(kind, dtype, text):
    return {w.split(":")[0]: (kind, [128, int(w.split(":")[1])], dtype) for w in text.split()}


SCRATCH = {}
SCRATCH.update(shapes("sbuf", "int32", "KID:3456 FUI:32 FSI:256 ZI:512 Z8:512 HI:32 OW:32 HT:16 HP:16 HR:256 RI:256 CI:1280"))
SCRATCH.update(shapes("sbuf", "uint16", "FUV:32 KU:512 OPU:16 JT:32 T1:32 OFF:32 PU:16 R1:256 SU:16 OF2:32 CT:16 EXL:16"))
SCRATCH.update(shapes("sbuf", "bfloat16", "VEC:3456 MRK:3456 FSB:256 NF:264 LASTF:256 EQ:256 KH:576 KL:576 MF:4096 VV:4096 DF:4096 AB:4096 "
                      "NS:4112 QV:4096 MQ:4096 CU:264 CV:256 CB:256 CD:264 XL:256 L2B:8 JW:768 JK:512 OO:512 LL:512 ZB:512 OHB:132 "
                      "STO:2320 NQ:256 ED:256 EO:1920 NK:512 NL:40 KB:32 H:256 M2:256 YH:512 YL:512 CM:4096 JR:256 "
                      "SND:2304 ARR:768 NEW:768 RPL:2304"))
SCRATCH.update(shapes("sbuf", "float32", "KF:512 D:4096 EM:4096 LG:256 XLI:256 SC:256 XC:256 T0:512 SN:132 RA:132 RB:132 R2:66 RQ:40 "
                      "RM:256 UH:256 NXT:768 NFX:256 FM:256 FL:256 PP:256 MD:256 OUTF:768 CF:1280 CR:1792 SM:976"))
VIEW = {}
for _w in ("L2:16 LT:8 PN:16 OP1:16 OP2:16 OP3:16 LEN:32 INV:32 OV:32 D2:32 O1:32 O2:32 O3:32 O4:32 IV:16 PF:16 P1:16 PM1:16 S1:16 "
           "S2:16 S3:16 NP:32 NP2:32 SF:32 ST:32 EN:32 PE1:32 X1:32 X2:32 KP:32 W0:32 VT:32 TOT:8 TOB:8 X3:32").split():
    _n, _k = _w.split(":")
    VIEW[_n] = ("SM", sum(x[2] for x in VIEW.values()), int(_k))
BANKS = ("BA", "BB", "BC", "BD", "BE", "BF", "BG", "BH")
SCRATCH.update({b: ("psum", [128, 512], "float32") for b in BANKS})
SEMAPHORES = ["qv", "qs", "qt", "qg"] + ["ld%d" % k for k in range(9)] + ["st%d" % k for k in range(4)] + ["ac%d" % k for k in range(len(CH))] + \
             ["%s%d" % (s, r) for s in ("ka", "ra", "lk", "lr") for r in range(RO)]


def rank_program(g, core, T, topo):
    me = T.rank_of(core)
    if me is None:
        return
    cores = list(T.cores)
    N = len(cores)

    def masks(src):
        s = cores[src]
        out = [d for d in range(N) if d != src and topo.chip(cores[d]) != topo.chip(s)]
        on = [d for d in range(N) if d != src and topo.chip(cores[d]) == topo.chip(s)]
        res = {}
        used = []
        for ds in (out, on):
            if ds:
                lst = [e for e in topo.engines(s, cores[ds[0]]) if e not in used]
                n = 1
                while n * 2 * len(ds) <= len(lst):
                    n *= 2
                for x, d in enumerate(ds):
                    res[d] = lst[x * n:(x + 1) * n]
                    used = used + res[d]
        return res

    queues = {"v": g.vector, "s": g.scalar, "t": g.tensor, "g": g, "y": g.sync}
    count = {}
    known = {q: {} for q in queues}
    waited = {}
    recs = {}
    finals = {}

    def dowaits(q, reads, writes):
        best = {}
        for regs, wr in ((reads, False), (writes, True)):
            for (b, lo, hi) in regs:
                for rec in recs.get(b, []):
                    if rec[0] < hi and lo < rec[1] and (wr or rec[2]):
                        s, v = rec[3]
                        if known[q].get(s, 0) < v and best.get(s, (0, None))[0] < v:
                            best[s] = (v, rec[4])
        for s in sorted(best, key=lambda s: -sum(best[s][1].values())):
            v, clk = best[s]
            if known[q].get(s, 0) >= v:
                continue
            queues[q].wait_ge(T.sem[s], v)
            waited[s] = max(waited.get(s, 0), v)
            known[q][s] = v
            for a, b in clk.items():
                known[q][a] = max(known[q].get(a, 0), b)

    def note(q, tok, reads, writes):
        clk = dict(known[q])
        clk[tok[0]] = max(clk.get(tok[0], 0), tok[1])
        for (b, lo, hi) in writes:
            recs[b] = [r for r in recs.get(b, []) if not (lo <= r[0] and r[1] <= hi)] + [(lo, hi, True, tok, clk)]
        for (b, lo, hi) in reads:
            recs[b] = [r for r in recs.get(b, []) if not (r[0] == lo and r[1] == hi and not r[2] and r[3][0] == tok[0])] + [(lo, hi, False, tok, clk)]
        finals[tok[0]] = max(finals.get(tok[0], 0), tok[1])

    def bankfix(reads, writes):
        w = [(x[0], 0, 512) if x[0] in BANKS else x for x in writes] + [(x[0], 0, 512) for x in reads if x[0] in BANKS]
        return [x for x in reads if x[0] not in BANKS], w

    def op(q, fn, reads, writes):
        reads, writes = bankfix(reads, writes)
        dowaits(q, reads, writes)
        s = "q" + q
        fn().then_inc(T.sem[s], 1)
        count[s] = count.get(s, 0) + 1
        note(q, (s, count[s]), reads, writes)

    def dma(q, sem, out, in_):
        dowaits(q, in_[1], out[1])
        queues[q].dma_start(out=out[0], in_=in_[0]).then_inc(T.sem[sem], 16)
        note(q, (sem, 16), in_[1], out[1])

    def addto(out, in_, sem):
        dowaits("g", in_[1], out[1])
        g.dma_start(out=out[0], in_=in_[0], accum_op=A.add).then_inc(T.sem[sem], 16)
        count[sem] = count.get(sem, 0) + 16
        note("g", (sem, count[sem]), in_[1], out[1])

    def R(name, lo=None, hi=None, step=None, p=None):
        if name in VIEW:
            name, at, n = VIEW[name]
            lo, hi = (at, at + n) if lo is None else (at + lo, at + hi)
        t = T[name]
        if lo is None:
            lo, hi = 0, t.shape[1]
        if p is not None:
            ap = t[p[0]:p[1], lo:hi]
        else:
            ap = t[:, lo:hi] if step is None else t[:, lo:hi:step]
        return (ap, [(name, lo, hi)])

    def I(win, off):
        return (win[0].indirect(off[0]), win[1] + off[1])

    def rg(*xs):
        return [r for x in xs if isinstance(x, tuple) for r in x[1]]

    def va(x):
        return x[0] if isinstance(x, tuple) else x

    def copy(out, in_):
        op("v", lambda: g.vector.tensor_copy(out=out[0], in_=in_[0]), rg(in_) + out[1][1:], out[1][:1])

    def tt(out, a, b, o):
        op("v", lambda: g.vector.tensor_tensor(out=out[0], in0=a[0], in1=b[0], op=o), rg(a, b), out[1])

    def ts(out, a, s1, o1, s2=None, o2=None):
        if o2 is None:
            op("v", lambda: g.vector.tensor_scalar(out=out[0], in0=a[0], scalar1=va(s1), scalar2=None, op0=o1), rg(a, s1), out[1])
        else:
            op("v", lambda: g.vector.tensor_scalar(out=out[0], in0=a[0], scalar1=va(s1), scalar2=va(s2), op0=o1, op1=o2), rg(a, s1, s2), out[1])

    def scan(out, d0, d1, init, o1, o2):
        op("v", lambda: g.vector.tensor_tensor_scan(out=out[0], data0=d0[0], data1=d1[0], initial=va(init), op0=o1, op1=o2), rg(d0, d1, init), out[1])

    def reduce(out, in_):
        op("v", lambda: g.vector.tensor_reduce(out=out[0], in_=in_[0], axis=AxisListType.X, op=A.add), in_[1], out[1])

    def fill(out, c):
        op("v", lambda: g.vector.memset(out[0], c), [], out[1])

    def act(out, in_, f, bias=0.0, scale=1.0):
        op("s", lambda: g.scalar.activation(out=out[0], in_=in_[0], func=f, bias=va(bias), scale=va(scale)), rg(in_, bias, scale), out[1])

    def mm(out, prs):
        rd, wr = bankfix(rg(*[x for p in prs for x in p[:2]]), out[1])
        ins = None
        for k, p in enumerate(prs):
            dowaits("t", rg(p[0], p[1]), wr)
            o = p[2] if len(p) > 2 else out
            ins = g.tensor.matmul(out=o[0], lhsT=p[0][0], rhs=p[1][0], start=(k == 0), stop=(k == len(prs) - 1))
        ins.then_inc(T.sem.qt, 1)
        count["qt"] = count.get("qt", 0) + 1
        note("t", ("qt", count["qt"]), rd, wr)

    def iota(out, pat, base, cm, flag=False):
        if flag:
            op("g", lambda: g.iota(out[0], pat, base, cm, allow_small_or_imprecise_dtypes=True), [], out[1])
        else:
            op("g", lambda: g.iota(out[0], pat, base, cm), [], out[1])

    def gfill(out, c):
        iota(out, [[0, out[1][0][2] - out[1][0][1]]], c, 0, True)

    dma("y", "ld0", R("FUI", 0, 16), (T.fu[:], []))
    dma("s", "ld1", R("FUI", 16, 32), (T.fv[:], []))
    dma("s", "ld2", R("FSI", 0, 256, p=(0, 8)), (T.fs[:], []))
    for k, (b, x) in enumerate((("KID", T.kids), ("VEC", T.vec), ("MRK", T.mark))):
        s0, s1 = "ld%d" % (3 + 2 * k), "ld%d" % (4 + 2 * k)
        g.sync.dma_start(out=T[b][0:64, :], in_=x[0:64, :]).then_inc(T.sem[s0], 16)
        g.scalar.dma_start(out=T[b][64:128, :], in_=x[64:128, :]).then_inc(T.sem[s1], 16)
        recs[b] = [(0, W, True, (s0, 16), {s0: 16}), (0, W, True, (s1, 16), {s1: 16})]
        finals[s0] = finals[s1] = 16

    free = {"CI": 0, "CF": 0, "CM": 0, "CR": 0}

    def new(buf, n):
        lo = free[buf]
        free[buf] = lo + (n + 15) // 16 * 16
        return R(buf, lo, lo + n)

    def part(m, a, b):
        return R(m[1][0][0], m[1][0][1] + a, m[1][0][1] + b)

    def win(m, i):
        return part(m, 15 - i, 143 - i)

    pI = new("CI", 1); cI = new("CI", 144); ktI = new("CI", 32); kdI = new("CI", 16); ksI = new("CI", 16); aI = new("CI", 256); exI = new("CI", 16)
    iota(pI, [[0, 1]], 0, 1)
    iota(cI, [[1, 144]], 0, 0)
    iota(ktI, [[16, 32]], 256, 0)
    iota(kdI, [[1, 16]], 512, 0)
    iota(ksI, [[16, 16]], SD, 0)
    iota(aI, [[1, 256]], 0, 0)
    iota(exI, [[1, 16]], 0, 0)
    gfill(R("MF"), 1)
    K1 = new("CR", 512); IQ = new("CR", 256)
    iota(K1, [[1, 512]], -4096, 0, True)
    iota(IQ, [[1, 256]], 0, 0, True)
    iota(R("JR"), [[1, 16], [16, 16]], 0, 0, True)
    gfill(R("STO"), -1)
    gfill(R("SND", 0, 256), -1)
    gfill(R("KH"), 0)
    gfill(R("KL"), 0)
    gfill(R("RPL", 256, 768), 0)
    for r in range(1, RO):
        gfill(R("SND", 768 * r, 768 * r + 256), -1)
        gfill(R("RPL", 768 * r + 256, 768 * r + 768), 0)
    pmI = new("CI", 1); pgI = new("CI", 1); cgI = new("CI", 144); cmI = new("CI", 144); amI = new("CI", 256)
    ts(pmI, pI, 15, A.bitwise_and)
    ts(pgI, pI, 4, A.arith_shift_right)
    ts(cgI, cI, 4, A.arith_shift_right)
    ts(cmI, cI, 15, A.bitwise_and)
    PM = new("CF", 1); PG = new("CF", 1); CG = new("CF", 144); CMF = new("CF", 144); PX = new("CF", 1)
    copy(PM, pmI); copy(PG, pgI); copy(CG, cgI); copy(CMF, cmI); copy(PX, pI)
    BLK = new("CM", 144); C15 = new("CM", 144); MST = new("CM", 144); G8 = new("CM", 8); R8 = new("CM", 128)
    ts(BLK, CG, PG, A.is_equal)
    ts(C15, CMF, 15.0, A.is_equal)
    tt(MST, BLK, C15, A.mult)
    ts(G8, part(cI, 0, 8), PG, A.is_equal)
    ts(R8, part(CG, 0, 128), PX, A.is_equal)
    ts(R("FSB", 0, 256, p=(0, 8)), R("FSI", 0, 256, p=(0, 8)), -1.0, A.mult, 1.0, A.add)
    r0 = R8[1][0][1]
    mm(R("BA", 0, 256), [((T.CM[0:8, r0:r0 + 128], R8[1]), R("FSB", 0, 256, p=(0, 8)))])
    fill(R("NF"), 0.0)
    copy(R("NF", 0, 256), R("BA", 0, 256))
    copy(R("FUV"), R("FUI"))
    WC = new("CF", 1)
    ts(WC, PM, -14.0, A.mult, 255.0, A.add)

    def scaled(src, by, n=144):
        m = new("CM", n)
        act(m, part(src, 0, n), AF.Identity, 0.0, by)
        return m
    MSL = scaled(MST, -float(2 ** 36)); MS = scaled(MST, 0.0625); MSC = scaled(MST, 2.0 ** -8); MSW = scaled(MST, WC)
    MS4 = scaled(MST, 4096.0); MSI = scaled(MST, PM)
    BW = scaled(BLK, WC, 128); BN = scaled(BLK, -1.0, 128); BI = scaled(BLK, PM, 128); G8S = scaled(G8, 0.0625, 8)
    B1 = part(BLK, 0, 128)
    DK = new("CF", 128); TMP = new("CF", 128); TM2 = new("CF", 128); CM1 = part(CMF, 0, 128)
    ts(DK, CM1, PM, A.subtract)

    def masked(o, c):
        m = new("CM", 128)
        ts(TMP, DK, c, o)
        tt(m, TMP, B1, A.mult)
        return m
    TRS = masked(A.is_gt, 0.0); TRI = masked(A.is_ge, 0.0); TGE = masked(A.is_le, 0.0); IDN = masked(A.is_equal, 0.0)
    S0 = masked(A.is_equal, 1.0); S1 = masked(A.is_equal, -15.0)
    TRN = new("CM", 128)
    ts(TMP, IDN, 65.0, A.mult)
    tt(TRN, TMP, TRI, A.subtract)
    TRX = new("CM", 128)
    ts(TMP, IDN, -4096.0, A.mult)
    tt(TRX, TRS, TMP, A.add)
    DA = new("CF", 128); DB = new("CF", 128)
    R4 = new("CR", 128); R4P = new("CR", 128); C4 = new("CR", 1)
    ts(DB, CM1, 0.0, A.is_equal)
    ts(DA, CM1, 0.0, A.is_gt, 0.25, A.mult)
    scan(R4, DA, DB, 0.0, A.mult, A.add)
    ts(TMP, CM1, 0.0, A.is_gt, 4.0, A.mult)
    scan(R4P, TMP, DB, 0.0, A.mult, A.add)
    tt(TM2, IDN, R4P, A.mult)
    reduce(C4, TM2)
    A1 = new("CM", 128); A0 = new("CM", 128); A2 = new("CM", 128)
    ts(TMP, R4, C4, A.mult, float(4 ** 16), A.mult)
    tt(A1, TMP, B1, A.mult)
    ts(TM2, TMP, float(4 ** 16), A.mult)
    tt(A0, TM2, TRS, A.mult)
    ts(TM2, TMP, float(4.0 ** -16), A.mult)
    tt(A2, TM2, TGE, A.mult)
    KT = new("CR", 32); KD = new("CR", 16); KS = new("CR", 16); PM16 = new("CF", 1); PM85 = new("CF", 1); ZR = new("CR", 256)
    MK = new("CR", 256); RS = new("CR", 132); QT = new("CR", 16)
    ts(KT, ktI, PM, A.add)
    ts(QT, part(KT, 0, 16), -256.0, A.add)
    ts(PM16, PM, 16.0, A.mult)
    ts(KD, kdI, PM16, A.add)
    ts(KS, ksI, PM, A.add)
    ts(PM85, PM, 8.5, A.add)
    ts(amI, aI, 15, A.bitwise_and)
    ts(MK, amI, PM, A.is_le, 4096.0, A.mult)
    ts(MK, MK, 1.0, A.add)
    copy(R("EXL"), exI)
    fill(ZR, 0.0)
    fill(RS, 1.0)
    for o in range(N):
        fill(part(RS, 33 * o, 33 * o + 1), 0.0)
    fill(R("OHB"), 0.0); fill(R("CD"), 0.0); fill(R("CU"), 0.0); fill(R("NL"), 0.0); fill(R("NS", 0, 16), 0.0)
    ts(R("CU", 1, 2), PM, 15.0, A.is_equal)

    def relay(outb, n, *parts):
        mm(R(outb, 0, n), [(win(m, i), R(b, lo + i, lo + 16 * n, 16)) for m, b, lo in parts for i in range(16)])

    def gv(c):
        a, n = CH[c]
        act(R("VV", a, a + n), I(R("VEC"), R("KU", 256 + a // 16, 256 + (a + n) // 16)), AF.Copy)

    def gq(c):
        a, n = CH[c]
        act(R("QV", a, a + n), I(R("MRK"), R("KU", 256 + a // 16, 256 + (a + n) // 16)), AF.Copy)

    def vphase():
        copy(R("KU", 256, 512), I(R("KID"), R("FUV", 16, 32)))
        copy(R("KU", 0, 256), I(R("KID"), R("FUV", 0, 16)))
        gv(0)
        gv(1)
        act(R("LASTF"), R("NF", 1, 257), AF.Identity, 1.0, -1.0)
        gfill(R("JW", 0, 512), 0)
        copy(R("MF", 0, P, 16), R("NF", 0, 256))
        for c, (a, n) in enumerate(CH):
            tt(R("DF", a, a + n), I(R("VEC"), R("KU", a // 16, (a + n) // 16)), R("VV", a, a + n), A.subtract)
            scan(R("D", a, a + n), R("MF", a, a + n), R("DF", a, a + n), R("D", a - 1, a) if a else 0.0, A.mult, A.add)
            if c + 2 < len(CH):
                gv(c + 2)
            elif c + 2 == len(CH):
                gq(0)
            act(R("AB", a, a + n), R("D", a, a + n), AF.Abs)
            j0, j1 = a // 16, (a + n) // 16
            mm(R("BC", j0, j1), [(win(MST, i), R("AB", a + i, a + n, 16)) for i in range(16)] + [(win(MSL, 15), R("LASTF", j0, j1))])

    def comp():
        copy(R("KF", 256, 512), R("KU", 256, 512))
        tt(R("EQ"), I(R("KID"), R("FUV", 0, 16)), R("KF", 256, 512), A.is_equal)
        ts(R("CU", 2, 258), R("BC", 0, 256), 0.0, A.is_le)
        mm(R("BD", 0, 256), [(A0, R("CU", 2, 258)), (A1, R("CU", 1, 257)), (A2, R("CU", 0, 256))])
        mm(R("BE", 0, 256), [(S0, R("CU", 2, 258)), (S1, R("CU", 1, 257))])
        yield
        tt(R("CV"), R("BD", 0, 256), R("CU", 2, 258), A.min)
        act(R("LG"), R("BD", 0, 256), AF.Ln, 0.25)
        act(R("XLI"), R("LG"), AF.Identity, 32.1 + RND, -1.0 / math.log(4.0))
        tt(R("CB"), R("BE", 0, 256), R("EQ"), A.mult)
        yield
        tt(R("CD", 1, 257), R("CV"), R("CB"), A.is_gt)
        mm(R("BH", 0, 16), [(win(MST, a), R("CD", 1 + 16 * a, 17 + 16 * a)) for a in range(16)])
        mm(R("BF", 0, 256), [(TRX, R("CD", 1, 257))])
        mm(R("BG", 0, 256), [(B1, R("CD", 0, 256))])
        yield
        scan(R("L2"), R("BH", 0, 16), part(ZR, 0, 16), 0.0, A.add, A.add)
        ts(R("PN"), R("BH", 0, 16), 0.0, A.is_equal, 8192.0, A.mult)
        copy(R("L2B", 0, 1), R("L2", 15, 16))
        tt(R("OP1"), R("BH", 0, 16), R("PN"), A.subtract)
        mm(R("BD", 0, 1), [(TRS, R("L2B", 0, 1))])
        yield
        tt(R("OP2"), R("L2"), R("OP1"), A.subtract)
        copy(R("LT", 0, 1), R("BD", 0, 1))
        yield
        ts(R("OP1"), R("OP2"), R("LT", 0, 1), A.add)
        ts(R("OP2"), R("OP1"), 512.0, A.is_ge, 8192.0, A.mult)
        tt(R("OP3"), R("OP1"), R("OP2"), A.max)
        tt(R("OP1"), R("OP3"), KD, A.min)
        copy(R("OPU"), R("OP1"))
        copy(I(R("JW"), R("OPU")), R("JR"))
        yield
        scan(R("JK"), R("JW", 0, 512), R("JW", 0, 512), 0.0, A.max, A.max)
        relay("BD", 32, (MS, "JK", 0))
        scan(R("SC"), R("BG", 0, 256), ZR, 0.0, A.add, A.add)
        yield
        act(R("XL"), R("XLI"), AF.Identity, -RND)
        copy(R("JT"), R("BD", 0, 32))
        yield
        tt(R("XC"), R("BF", 0, 256), R("SC"), A.add)
        yield
        tt(R("OO"), I(R("XC"), R("JT")), K1, A.is_equal)
        tt(R("LL"), I(R("XL"), R("JT")), R("OO"), A.mult)
        relay("BE", 32, (MST, "JK", 0), (MSI, "OO", 0))
        relay("BF", 32, (MST, "LL", 0))
        mm(R("BG", 0, 512), [(B1, R("JK")), (BI, R("OO")), (BN, R("LL"))])
        yield
        copy(R("T1"), R("BE", 0, 32))
        copy(R("LEN"), R("BF", 0, 32))
        ts(R("INV"), R("BF", 0, 32), 0.0, A.is_equal, 8.0, A.mult)
        act(R("T0"), R("BG", 0, 512), AF.Identity, 9.5)
        yield

    def qphase():
        for c in range(1, len(CH)):
            gq(c)
        banks = ("BA", "BB", "BC")
        rc = 0
        for c, (a, n) in enumerate(CH):
            tt(R("MQ", a, a + n), I(R("MRK"), R("KU", a // 16, (a + n) // 16)), R("QV", a, a + n), A.max)
            addto(R("D", a, a + n), R("MQ", a, a + n), "ac%d" % c)
            for _ in range(2 if c >= 2 else 0):
                b = banks[rc % 3]
                mm(R(b, 0, 512), [(B1, R("AB", 512 * rc, 512 * rc + 512))])
                act(R("NS", 512 * rc + 1, 512 * rc + 513), R(b, 0, 512), AF.Sign)
                rc += 1
            yield
        tt(R("NS", 0, P, 16), R("NS", 0, P, 16), R("NF", 0, 256), A.mult)
        yield
        for a in range(0, P, 2048):
            scan(R("EM", a, a + 2048), R("NS", a, a + 2048), R("D", a, a + 2048), R("EM", a - 1, a) if a else 0.0, A.mult, A.add)
            yield

    def fused(src, dst, lsem, rsem):
        m = masks(me)
        tr, rd, tot = [], [], 0
        for d in range(N):
            if d != me:
                rid, pid = topo.addr(cores[d])[:2]
                x = src(d)
                rd += x[1]
                tot += len(m[d])
                tr.append(RemoteDMATransfer(dst_ids=[DstId(rid=rid, pnc=pid)], dma_engine_mask=sum(1 << e for e in m[d]), remote_sem=T.sem[rsem], src=x[0], dst=dst[0]))
        dowaits("g", rd, [])
        g.remote_dma_fused(tr, local_sem=T.sem[lsem])
        note("g", (lsem, tot), rd, [])

    def landed(sem, buf, base):
        tot = sum(len(masks(s)[me]) for s in range(N) if s != me)
        for s in range(N):
            if s != me:
                recs.setdefault(buf, []).append((base + CAP * s, base + CAP * (s + 1), True, (sem, tot), {sem: tot}))
        finals[sem] = tot

    def keys(r):
        copy(R("ZI"), I(R("EM"), R("T1")))
        ts(R("Z8"), R("ZI"), 255, A.bitwise_and)
        copy(R("ZB"), R("Z8"))
        relay("BD", 32, (MSW, "ZB", 0))
        copy(R("HI"), R("BD", 0, 32))
        ts(R("OW"), R("HI"), 3, A.bitwise_and)
        tt(R("OV"), R("OW"), R("INV"), A.add)
        for o in range(N):
            ts(R("OHB", 33 * o + 1, 33 * o + 33), R("OV"), float(o), A.is_equal)
        mm(R("BE", 0, 132), [(BN, R("OHB"))])
        mm(R("BF", 0, 132), [(TRN, R("OHB"))])
        ts(R("D2"), R("OV"), 64.0, A.mult, 64.0, A.add)
        scan(R("SN"), RS, R("BE", 0, 132), 0.0, A.mult, A.add)
        tt(R("RA", 1, 132), R("BF", 1, 132), R("SN", 0, 131), A.add)
        tt(R("RB", 1, 132), R("RA", 1, 132), R("OHB", 1, 132), A.mult)
        tt(R("R2", 1, 66), R("RB", 1, 66), R("RB", 67, 132), A.add)
        tt(R("RQ", 1, 33), R("R2", 1, 33), R("R2", 34, 66), A.add)
        ts(R("O1"), R("RQ", 1, 33), 0.0, A.is_le, 4096.0, A.mult)
        tt(R("O2"), R("D2"), R("RQ", 1, 33), A.subtract)
        tt(R("O3"), R("O2"), R("O1"), A.max)
        tt(R("O4"), R("O3"), KT, A.min)
        copy(R("OFF"), R("O4"))
        b, c = 768 * r, 256 * r + CAP * me
        copy(I(R("SND", b, b + 768), R("OFF")), R("ZB"))
        fused(lambda d: R("SND", b + CAP * d, b + CAP * d + CAP), R("ARR", c, c + CAP), "lk%d" % r, "ka%d" % r)
        act(R("ARR", c, c + CAP), R("SND", b + CAP * me, b + CAP * me + CAP), AF.Copy)
        fill(R("NXT", 0, 256), 1.0)
        copy(R("KF", 0, 256), R("KU", 0, 256))
        for k in range(2):
            ts(R("KH", TW * k, TW * k + 256), R("KU", 256 * k, 256 * k + 256), MAG, A.add, MAG, A.subtract)
            tt(R("KL", TW * k, TW * k + 256), R("KF", 256 * k, 256 * k + 256), R("KH", TW * k, TW * k + 256), A.subtract)
        landed("ka%d" % r, "ARR", 256 * r)

    def owner(r):
        b = 256 * r
        arr = R("ARR", b, b + 256)
        mm(R("BH", 0, 256), [(BW, arr)])
        relay("BG", 16, (MSW, "ARR", b))
        copy(R("HR"), R("BH", 0, 256))
        ts(R("RI"), R("HR"), 2, A.arith_shift_right, TS - 1, A.bitwise_and)
        copy(R("HT"), R("BG", 0, 16))
        ts(R("HP"), R("HT"), 2, A.arith_shift_right, TS - 1, A.bitwise_and)
        ts(R("IV"), R("HT"), 0.0, A.is_lt, float(TS), A.mult)
        tt(R("PF"), R("HP"), R("IV"), A.max)
        copy(R("PU"), R("PF"))
        tt(R("NQ"), I(R("STO"), R("PU")), arr, A.not_equal)
        relay("BD", 16, (MS4, "NQ", 0))
        mm(R("BE", 0, 256), [(B1, R("NQ"))])
        ts(R("R1"), R("RI"), 1.0, A.add)
        tt(R("RM"), R("RI"), MK, A.add)
        ts(R("P1"), R("PF"), 1.0, A.add)
        tt(R("PM1"), R("BD", 0, 16), R("P1"), A.min)
        tt(R("ED"), I(R("PM1"), R("EXL")), R("RM"), A.is_equal)
        eo = [(B1, R("ED"))]
        lo = 0
        for m in range(15):
            n = 240 - 16 * m
            ts(R("EO", lo, lo + n), R("R1", 16 * m + 16, 256), R("PM1", m, m + 1), A.is_equal)
            eo.append((B1, R("EO", lo, lo + n), R("BF", 16 * m + 16, 256)))
            lo += n
        ts(R("UH"), R("BE", 0, 256), 1.0, A.min, 0.5, A.mult)
        mm(R("BF", 0, 256), eo)
        tt(R("NEW", b, b + 256), R("UH"), R("BF", 0, 256), A.is_gt)
        rb = 768 * r + CAP * me
        fused(lambda d: R("NEW", b + CAP * d, b + CAP * d + CAP), R("RPL", rb, rb + CAP), "lr%d" % r, "ra%d" % r)
        act(R("RPL", rb, rb + CAP), R("NEW", b + CAP * me, b + CAP * me + CAP), AF.Copy)
        landed("ra%d" % r, "RPL", 768 * r)
        relay("BG", 16, (MS, "NEW", b))
        ts(R("S1"), R("BG", 0, 16), 0.0, A.is_equal, 8192.0, A.mult)
        tt(R("S2"), R("S1"), R("PF"), A.max)
        tt(R("S3"), R("S2"), KS, A.min)
        copy(R("SU"), R("S3"))
        copy(I(R("STO"), R("SU")), arr)
        if r == RO - 1:
            dma("y", "st0", (T.yt[:], []), R("STO", 0, TS))

    def nextfront(r):
        b = 768 * r
        last = r == RO - 1
        act(R("NK", 0, 224), I(R("RPL", b, b + 768), part(R("OFF"), 0, 14)), AF.Copy)
        copy(R("NK", 224, 512), I(R("RPL", b, b + 768), part(R("OFF"), 14, 32)))
        relay("BH", 32, (MS, "NK", 0))
        tt(R("NL", 1, 33), R("BH", 0, 32), R("LEN"), A.mult)
        mm(R("BD", 0, 32), [(B1, R("NL", 0, 32))])
        mm(R("BE", 0, 32), [(TRS, R("NL", 1, 33))])
        ts(R("NP"), R("NL", 1, 33), 0.0, A.is_equal, 2048.0, A.mult)
        scan(R("SF"), R("BD", 0, 32), part(ZR, 0, 32), 0.0, A.add, A.add)
        tt(R("NP2"), R("NP"), R("NL", 1, 33), A.add)
        tt(R("ST"), R("BE", 0, 32), R("SF"), A.add)
        tt(R("EN"), R("ST"), R("NP2"), A.add)
        ts(R("PE1"), R("EN"), 256.0, A.is_gt, 32768.0, A.mult)
        ts(R("KP"), R("EN"), 256.0, A.is_le)
        tt(R("X1"), R("ST"), R("PE1"), A.max)
        tt(R("KB"), R("KP"), R("NL", 1, 33), A.mult)
        tt(R("X2"), R("X1"), KT, A.min)
        mm(R("BC", 0, 32), [(B1, R("KB"))])
        copy(R("OF2"), R("X2"))
        op("s", lambda: g.scalar.activation(out=R("X3")[0], in_=T.BC[:, 0:32], func=AF.Copy, accum_out=R("TOT", 0, 1)[0]),
           [("BC", 0, 32)], R("X3")[1] + R("TOT", 0, 1)[1])
        if not last:
            act(R("TOB", 0, 1), R("TOT", 0, 1), AF.Identity, 0.5, -1.0)
            for k in range(2):
                act(R("VT", 16 * k, 16 * k + 16), QT, AF.Sign, R("TOB", 0, 1))
            act(R("VT"), R("VT"), AF.Relu, 0.0, -1.0)
        else:
            act(R("TOB", 0, 1), R("TOT", 0, 1), AF.Identity, 16384.0, -32768.0)
            act(R("FM"), IQ, AF.Relu, R("TOB", 0, 1), 32768.0)
        copy(I(R("NXT"), R("OF2")), R("T0"))
        ts(R("NFX"), R("NXT", 0, 256), 1.0, A.is_equal)
        scan(R("PP"), R("NFX"), R("NXT", 0, 256), 0.0, A.mult, A.add)
        ts(R("H"), R("PP"), MAG, A.add, MAG + 16.0, A.subtract)
        relay("BF", 16, (MSC, "H", 0))
        if last:
            tt(R("PP"), R("PP"), R("FM"), A.max)
        tt(R("MD"), R("PP"), R("H"), A.subtract)
        ts(R("M2"), R("MD"), PM85, A.is_equal)
        copy(R("CT"), R("BF", 0, 16))
        for y, k0 in (("YH", "KH"), ("YL", "KL")):
            for k in range(2):
                tt(R(y, 256 * k, 256 * k + 256), I(R(k0, TW * k, TW * k + TW), R("CT")), R("M2"), A.mult)
        if not last:
            relay("BG", 32, (MST, "YH", 0), (MST, "YL", 0))
        else:
            mm((T.BG[0:8, 0:512], [("BG", 0, 512)]), [(G8, R("YH")), (G8, R("YL"))])
        ts(R("FL"), IQ, R("TOT", 0, 1), A.is_lt)
        tt(R("NF", 0, 256), R("FL"), R("NFX"), A.mult)
        if not last:
            tt(R("W0"), R("BG", 0, 32), R("VT"), A.mult)
            copy(R("FUV"), R("W0"))
        else:
            mm((T.BH[0:8, 0:256], [("BH", 0, 512)]), [(G8S, R("NF", 0, 256))])
            copy(R("OUTF", 0, 512, p=(0, 8)), (T.BG[0:8, 0:512], [("BG", 0, 512)]))
            dma("y", "st1", (T.yu[:], []), R("OUTF", 0, 256, p=(0, 8)))
            dma("s", "st2", (T.yv[:], []), R("OUTF", 256, 512, p=(0, 8)))
            ts(R("OUTF", 512, 768, p=(0, 8)), (T.BH[0:8, 0:256], [("BH", 0, 512)]), -1.0, A.mult, 1.0, A.add)
            dma("s", "st3", (T.ys[:], []), R("OUTF", 512, 768, p=(0, 8)))

    for r in range(RO):
        vphase()
        two = {"B": qphase(), "A": comp()}
        for x in ORDER:
            next(two[x], None)
        for x in two.values():
            for _ in x:
                pass
        keys(r)
        owner(r)
        nextfront(r)
    for s in sorted(finals):
        if waited.get(s, 0) < finals[s]:
            g.wait_ge(T.sem[s], finals[s])
